import numpy as np
import ml_dtypes


def mxq(x, axis, fmt="e4m3"):
    dtype, down = {"e4m3": (ml_dtypes.float8_e4m3fn, 7), "e5m2": (ml_dtypes.float8_e5m2, 14)}[fmt]
    v = np.moveaxis(np.asarray(x, np.float32).astype(ml_dtypes.bfloat16).astype(np.float64), axis, -1)
    blocks = v.reshape(v.shape[:-1] + (-1, 32))
    amax = np.abs(blocks).max(-1, keepdims=True)
    byte = np.maximum(np.where(amax > 0, np.frexp(amax)[1] - 1 + 127, 0) - down, 1)
    scale = np.exp2(byte - 127.0)
    codes = (blocks / scale).astype(np.float32).astype(dtype).astype(np.float64)
    return np.moveaxis((codes * scale).reshape(v.shape), -1, axis)


WIDE = False


def mx_kscale(k):
    if not WIDE:
        return np.ones(k)
    levels = np.array([10, -10, 5, -5, 0])
    if k % 512:
        return np.exp2(np.random.permutation(np.resize(levels, k // 32))).repeat(32)
    a = np.empty((k // 512, 16))
    for p in range(k // 512):
        a[p, :8] = np.random.permutation(np.resize(levels, 8))
        for g in range(8):
            far = levels[np.abs(levels - a[p, g]) >= 10]
            a[p, g + 8] = far[np.random.randint(len(far))]
    return np.exp2(a.ravel()).repeat(32)


def f64(x):
    return np.asarray(x).astype(np.float64)


def striped(idx):
    return np.tile(idx.reshape(-1, 16).T, (8, 1)).astype(np.uint16)


def unstriped(offs):
    return offs[:16].T.reshape(-1).astype(np.int64)


def pack_weight(w):
    k, n = w.shape
    w = f64(np.asarray(w, np.float32).astype(ml_dtypes.bfloat16)).reshape(k // 32, 32, n)
    amax = np.abs(w).max(1)
    byte = np.clip(np.where(amax > 0, np.frexp(amax)[1] - 1 + 127 - 7, 1), 1, 254)
    scaled = (w * np.exp2(127.0 - byte)[:, None, :]).reshape(k, n).astype(np.float32)
    words = np.ascontiguousarray(scaled.reshape(k // 512, 128, 4, n).transpose(0, 1, 3, 2)).astype(ml_dtypes.float8_e4m3fn).view(np.uint8)
    return words, np.ascontiguousarray(byte.astype(np.uint8).reshape(k // 512, 16, n))


def unpack_weight(words, scales):
    g, p, n, _ = words.shape
    vals = np.ascontiguousarray(words).view(ml_dtypes.float8_e4m3fn).astype(np.float64) * np.repeat(np.exp2(scales.astype(np.float64) - 127.0), 8, axis=1)[..., None]
    return vals.transpose(0, 1, 3, 2).reshape(g * 512, n)


E2M1 = np.array([0.0, 0.5, 1.0, 1.5, 2.0, 3.0, 4.0, 6.0, -0.0, -0.5, -1.0, -1.5, -2.0, -3.0, -4.0, -6.0])


def pack_fp4(w):
    k, n = w.shape
    w = f64(np.asarray(w, np.float32).astype(ml_dtypes.bfloat16)).reshape(k // 32, 32, n)
    amax = np.abs(w).max(1)
    mant, ex = np.frexp(amax / 6.0)
    byte = np.clip(np.where(amax > 0, np.where(mant > 0.5, ex, ex - 1) + 127, 1), 1, 254)
    scaled = (w * np.exp2(127.0 - byte)[:, None, :]).reshape(k, n).astype(np.float32)
    c = np.ascontiguousarray(scaled.reshape(k // 512, 128, 4, n).transpose(0, 1, 3, 2)).astype(ml_dtypes.float4_e2m1fn).view(np.uint8) & 0xF
    words = (c[..., 0::2] | (c[..., 1::2] << 4)).reshape(k // 512, 128, 2 * n)
    return np.ascontiguousarray(words), np.ascontiguousarray(byte.astype(np.uint8).reshape(k // 512, 16, n))


def unpack_fp4(words, scales):
    g, _, n = scales.shape
    words = np.ascontiguousarray(words).reshape(g, 128, n, 2)
    nib = np.empty((g, 128, n, 4), np.uint8)
    nib[..., 0::2] = words & 0xF
    nib[..., 1::2] = words >> 4
    vals = E2M1[nib] * np.repeat(np.exp2(scales.astype(np.float64) - 127.0), 8, axis=1)[..., None]
    return vals.transpose(0, 1, 3, 2).reshape(g * 512, n)


def planes(y):
    n, m = y.shape
    v = y.astype(np.float32).astype(ml_dtypes.bfloat16).astype(np.float64).reshape(n // 32, 32, m)
    top = np.abs(v).max(1)
    byte = np.clip(np.where(top > 0, np.frexp(top)[1] - 1 + 127 - 7, 1), 1, 254)
    codes = (v * np.exp2(127.0 - byte)[:, None, :]).reshape(n, m).astype(np.float32).astype(ml_dtypes.float8_e4m3fn).view(np.uint8)
    words = codes.reshape(n // 512, 128, 4, m).transpose(0, 1, 3, 2)
    return np.ascontiguousarray(words), np.ascontiguousarray(byte.astype(np.uint8).reshape(n // 512, 16, m))


K, T, S, H = 512, 1024, 512, 512


def setup_inputs():
    n = np.random.standard_normal
    s = mx_kscale(K)[:, None]
    u = mx_kscale(H)
    packed_xT = pack_weight(n((K, T)) * s)
    packed_w2 = pack_fp4(n((H, H)) / np.sqrt(H) / u[:, None])
    return {
        "x_words": packed_xT[0],
        "x_scales": packed_xT[1],
        "w1": (n((K, H)) / np.sqrt(K) / s * u).astype(np.float32),
        "w2_words": packed_w2[0],
        "w2_scales": packed_w2[1],
        "offs": striped(np.random.permutation(T)[:S]),
    }


def reference(x_words, x_scales, w1, w2_words, w2_scales, offs):
    xq = unpack_weight(x_words, x_scales)[:, unstriped(offs)]
    h = mxq(f64(w1), 0, "e4m3").T @ xq
    z = h - h.mean(axis=1, keepdims=True)
    out_0 = unpack_fp4(w2_words, w2_scales).T @ mxq(z, 0, "e4m3")
    return (out_0,) + planes(out_0)

@@ -1,0 +1,182 @@
+from contextlib import ExitStack
+
+import concourse.mybir as mybir
+
+K, T, S, H = 512, 1024, 512, 512
+FLOPS = 2 * K * H * S + 2 * H * H * S
+
+F32 = mybir.dt.float32
+BF16 = mybir.dt.bfloat16
+I32 = mybir.dt.int32
+U32 = mybir.dt.uint32
+U16 = mybir.dt.uint16
+U8 = mybir.dt.uint8
+FP8X4 = mybir.dt.float8_e4m3fn_x4
+FP4X4 = mybir.dt.float4_e2m1fn_x4
+ALU = mybir.AluOpType
+COPY = mybir.ActivationFunctionType.Copy
+AXIS_X = mybir.AxisListType.X
+
+P = 128
+PACK = 4
+CHUNK = 128
+CHUNKS = S // CHUNK
+HALF = H // 2
+M_HALF = HALF // PACK
+M_SCALAR = (64, 18)
+GATHERS = ((0, 128), (128, 256), (256, 512))
+
+
+def tile_picked_deepset_none_po_kernel(
+    tc, x_words, x_scales, w1, w2_words, w2_scales, offs, out_0, out_1, out_2
+):
+    nc = tc.nc
+    with ExitStack() as ctx:
+        pool = ctx.enter_context(tc.tile_pool(name="sbuf", bufs=1))
+        psum = ctx.enter_context(tc.psum_pool(name="psum", bufs=1))
+
+        offsets = pool.tile([P, S // 16], U16, name="offsets")
+        x_scale_table = pool.tile([P, T], U8, name="x_scale_table", align_bytes=64)
+        x_word_table = pool.tile([P, T], U32, name="x_word_table", align_bytes=64)
+        w1_raw = [pool.tile([P, PACK, HALF], F32, name="w1_raw%d" % h, align_bytes=64) for h in range(2)]
+
+        nc.vector.memset(x_scale_table[:].bitcast(I32), 0)
+        nc.sync.dma_start(offsets[:], offs)
+        w1_rows = w1.rearrange("(p j) c -> p j c", j=PACK)
+        nc.sync.dma_start(w1_raw[0][:], w1_rows[:, :, :HALF])
+        for q in range(4):
+            nc.sync.dma_start(
+                x_scale_table[32 * q : 32 * q + 4, :].bitcast(I32), x_scales[0, 4 * q : 4 * q + 4, :].bitcast(I32)
+            )
+        nc.sync.dma_start(w1_raw[1][:], w1_rows[:, :, HALF:])
+        nc.sync.dma_start(x_word_table[:].bitcast(I32), x_words[0].rearrange("p n r -> p (n r)").bitcast(I32))
+        w2_raw_scales = pool.tile([P, H], U8, name="w2_raw_scales", align_bytes=64)
+        w2_raw = pool.tile([P, 2 * H], U8, name="w2_raw", align_bytes=64)
+        nc.gpsimd.memset(w2_raw_scales[:].bitcast(I32), 0)
+        nc.sync.dma_start(w2_raw[:].bitcast(I32), w2_words[0].bitcast(I32))
+        for q in range(4):
+            nc.sync.dma_start(
+                w2_raw_scales[32 * q : 32 * q + 4, :].bitcast(I32), w2_scales[0, 4 * q : 4 * q + 4, :].bitcast(I32)
+            )
+
+
+        x_scale = pool.tile([P, S], U8, name="x_scale", align_bytes=64)
+        nc.vector.tensor_copy(x_scale[:], x_scale_table[:].indirect(offsets[:]))
+
+        w1_grouped = pool.tile([P, PACK * H], BF16, name="w1_grouped", align_bytes=64)
+        w1_dst = w1_grouped[:].rearrange("p (t m j) -> p m j t", t=PACK, j=PACK)
+        for h in range(2):
+            src = w1_raw[h][:].rearrange("p j (m t) -> p m j t", t=PACK)
+            m0, cut = h * M_HALF, M_SCALAR[h]
+            nc.scalar.activation(w1_dst[:, m0 : m0 + cut], src[:, :cut], COPY)
+            if cut < M_HALF:
+                nc.vector.tensor_copy(w1_dst[:, m0 + cut : m0 + M_HALF], src[:, cut:])
+        w1_codes = pool.tile([P, H], U32, name="w1_codes", align_bytes=64)
+        w1_scale = pool.tile([P, H], U8, name="w1_scale", align_bytes=64)
+        x_codes = pool.tile([P, S], U32, name="x_codes", align_bytes=64)
+
+        def quantize_w1(t):
+            nc.vector.quantize_mx(
+                out=w1_codes[:, t * P : (t + 1) * P].bitcast(FP8X4),
+                scales=w1_scale[:, t * P : (t + 1) * P],
+                in_=w1_grouped[:, t * PACK * P : (t + 1) * PACK * P],
+            )
+
+        def gather_words(a, b):
+            nc.vector.tensor_copy(x_codes[:, a:b], x_word_table[:].indirect(offsets[:, a // 16 : b // 16]))
+
+        quantize_w1(0)
+        gather_words(*GATHERS[0])
+        for t in range(1, PACK):
+            quantize_w1(t)
+        for a, b in GATHERS[1:]:
+            gather_words(a, b)
+
+        w2_codes = pool.tile([P, 2 * H], U8, name="w2_codes", align_bytes=64)
+        w2_scale = pool.tile([P, H], U8, name="w2_scale", align_bytes=64)
+        nc.vector.tensor_copy(
+            w2_codes[:].rearrange("p (t m b) -> p t m b", t=PACK, b=2),
+            w2_raw[:].rearrange("p (m t b) -> p t m b", t=PACK, b=2),
+        )
+        nc.vector.tensor_copy(
+            w2_scale[:].rearrange("p (t m) -> p t m", t=PACK), w2_raw_scales[:].rearrange("p (m t) -> p t m", t=PACK)
+        )
+
+        h_banks = [psum.tile([P, PACK, CHUNK], F32, name="h_bank%d" % c) for c in range(CHUNKS)]
+        partial = pool.tile([P, CHUNKS, PACK], F32, name="partial")
+        unread = pool.tile([P, 2, PACK, CHUNK], BF16, name="unread")
+        for c in range(CHUNKS):
+            cols = slice(c * CHUNK, (c + 1) * CHUNK)
+            for t in range(PACK):
+                nc.tensor.matmul_mx(
+                    out=h_banks[c][:, t, :],
+                    lhsT=w1_codes[:, t * P : (t + 1) * P].bitcast(FP8X4),
+                    lhsT_scale=w1_scale[:, t * P : (t + 1) * P],
+                    rhs=x_codes[:, cols].bitcast(FP8X4),
+                    rhs_scale=x_scale[:, cols],
+                    start=True,
+                    stop=True,
+                )
+            if c < 2:
+                for t in range(PACK):
+                    nc.scalar.activation(unread[:, c, t, :], h_banks[c][:, t, :], COPY, accum_out=partial[:, c, t : t + 1])
+            else:
+                nc.vector.tensor_reduce(partial[:, c, :], h_banks[c][:], AXIS_X, ALU.add)
+        total = pool.tile([P, PACK], F32, name="total")
+        nc.vector.tensor_reduce(total[:], partial[:].rearrange("p c t -> p t c"), AXIS_X, ALU.add)
+
+        z_codes = pool.tile([P, S], U32, name="z_codes", align_bytes=64)
+        z_scale = pool.tile([P, S], U8, name="z_scale", align_bytes=64)
+        y_codes = pool.tile([P, S], U32, name="y_codes", align_bytes=64)
+        y_scale = pool.tile([P, S], U8, name="y_scale", align_bytes=64)
+        y_banks = [psum.tile([P, PACK, CHUNK], F32, name="y_bank%d" % c) for c in range(CHUNKS)]
+        for c in range(CHUNKS):
+            cols = slice(c * CHUNK, (c + 1) * CHUNK)
+            z = pool.tile([P, CHUNK, PACK], BF16, name="z%d" % c, align_bytes=64)
+            nc.vector.scalar_tensor_tensor(
+                z[:],
+                total[:].unsqueeze(1).to_broadcast([P, CHUNK, PACK]),
+                -1.0 / S,
+                h_banks[c][:].rearrange("p t n -> p n t"),
+                ALU.mult,
+                ALU.add,
+            )
+            nc.vector.quantize_mx(
+                out=z_codes[:, cols].bitcast(FP8X4), scales=z_scale[:, cols], in_=z[:].rearrange("p n t -> p (n t)")
+            )
+            for t in range(PACK):
+                nc.tensor.matmul_mx(
+                    out=y_banks[c][:, t, :],
+                    lhsT=w2_codes[:, 2 * t * P : 2 * (t + 1) * P].bitcast(FP4X4),
+                    lhsT_scale=w2_scale[:, t * P : (t + 1) * P],
+                    rhs=z_codes[:, cols].bitcast(FP8X4),
+                    rhs_scale=z_scale[:, cols],
+                    start=True,
+                    stop=True,
+                )
+
+        out_rows = out_0.rearrange("(p t) n -> p t n", t=PACK)
+        out_words = out_1[0].rearrange("p n r -> p (n r)").bitcast(I32)
+        for c in range(CHUNKS):
+            cols = slice(c * CHUNK, (c + 1) * CHUNK)
+            y = pool.tile([P, PACK, CHUNK], F32, name="y%d" % c, align_bytes=64)
+            nc.scalar.copy(y[:], y_banks[c][:])
+            nc.sync.dma_start(out_rows[:, :, cols], y[:])
+            y_grouped = pool.tile([P, CHUNK, PACK], BF16, name="y_grouped%d" % c, align_bytes=64)
+            if c == 0:
+                nc.scalar.copy(y_grouped[:], y_banks[c][:].rearrange("p t n -> p n t"))
+            else:
+                nc.vector.tensor_copy(
+                    y_grouped[:].rearrange("p (a i) t -> p a t i", i=4), y[:].rearrange("p t (a i) -> p a t i", i=4)
+                )
+            nc.vector.quantize_mx(
+                out=y_codes[:, cols].bitcast(FP8X4),
+                scales=y_scale[:, cols],
+                in_=y_grouped[:].rearrange("p n t -> p (n t)"),
+            )
+            if c % 2 == 1:
+                pair = slice((c - 1) * CHUNK, (c + 1) * CHUNK)
+                nc.sync.dma_start(out_words[:, pair], y_codes[:, pair].bitcast(I32))
+        for q in range(4):
+            queue = nc.scalar if q % 2 == 0 else nc.sync
+            queue.dma_start(out_2[0, 4 * q : 4 * q + 4, :].bitcast(I32), y_scale[32 * q : 32 * q + 4, :].bitcast(I32))

@@ -129,54 +129,72 @@ def tile_picked_deepset_none_po_kernel(
         z_scale = pool.tile([P, S], U8, name="z_scale", align_bytes=64)
         y_codes = pool.tile([P, S], U32, name="y_codes", align_bytes=64)
         y_scale = pool.tile([P, S], U8, name="y_scale", align_bytes=64)
-        y_banks = [psum.tile([P, PACK, CHUNK], F32, name="y_bank%d" % c) for c in range(CHUNKS)]
-        for c in range(CHUNKS):
-            cols = slice(c * CHUNK, (c + 1) * CHUNK)
-            z = pool.tile([P, CHUNK, PACK], BF16, name="z%d" % c, align_bytes=64)
+        z = [pool.tile([P, CHUNK, PACK], BF16, name="z%d" % c, align_bytes=64) for c in range(CHUNKS)]
+        y = [pool.tile([P, PACK, CHUNK], F32, name="y%d" % c, align_bytes=64) for c in range(CHUNKS)]
+        y_grouped = [pool.tile([P, CHUNK, PACK], BF16, name="y_grouped%d" % c, align_bytes=64) for c in range(CHUNKS)]
+        out_rows = out_0.rearrange("(p t) n -> p t n", t=PACK)
+        out_words = out_1[0].rearrange("p n r -> p (n r)").bitcast(I32)
+
+        def center(c, a, b):
             nc.vector.scalar_tensor_tensor(
-                z[:],
-                total[:].unsqueeze(1).to_broadcast([P, CHUNK, PACK]),
+                z[c][:, a:b, :],
+                total[:].unsqueeze(1).to_broadcast([P, b - a, PACK]),
                 -1.0 / S,
-                h_banks[c][:].rearrange("p t n -> p n t"),
+                h_banks[c][:, :, a:b].rearrange("p t n -> p n t"),
                 ALU.mult,
                 ALU.add,
             )
-            nc.vector.quantize_mx(
-                out=z_codes[:, cols].bitcast(FP8X4), scales=z_scale[:, cols], in_=z[:].rearrange("p n t -> p (n t)")
-            )
-            for t in range(PACK):
-                nc.tensor.matmul_mx(
-                    out=y_banks[c][:, t, :],
-                    lhsT=w2_codes[:, 2 * t * P : 2 * (t + 1) * P].bitcast(FP4X4),
-                    lhsT_scale=w2_scale[:, t * P : (t + 1) * P],
-                    rhs=z_codes[:, cols].bitcast(FP8X4),
-                    rhs_scale=z_scale[:, cols],
-                    start=True,
-                    stop=True,
-                )
 
-        out_rows = out_0.rearrange("(p t) n -> p t n", t=PACK)
-        out_words = out_1[0].rearrange("p n r -> p (n r)").bitcast(I32)
-        for c in range(CHUNKS):
+        def second_layer(c):
             cols = slice(c * CHUNK, (c + 1) * CHUNK)
-            y = pool.tile([P, PACK, CHUNK], F32, name="y%d" % c, align_bytes=64)
-            nc.scalar.copy(y[:], y_banks[c][:])
-            nc.sync.dma_start(out_rows[:, :, cols], y[:])
-            y_grouped = pool.tile([P, CHUNK, PACK], BF16, name="y_grouped%d" % c, align_bytes=64)
-            if c == 0:
-                nc.scalar.copy(y_grouped[:], y_banks[c][:].rearrange("p t n -> p n t"))
-            else:
-                nc.vector.tensor_copy(
-                    y_grouped[:].rearrange("p (a i) t -> p a t i", i=4), y[:].rearrange("p t (a i) -> p a t i", i=4)
-                )
+            nc.vector.quantize_mx(
+                out=z_codes[:, cols].bitcast(FP8X4), scales=z_scale[:, cols], in_=z[c][:].rearrange("p n t -> p (n t)")
+            )
+            per_bank = PACK // 2 if c == CHUNKS - 1 else PACK
+            for t0 in range(0, PACK, per_bank):
+                bank = psum.tile([P, per_bank, CHUNK], F32, name="y_bank", bufs=4)
+                for t in range(t0, t0 + per_bank):
+                    nc.tensor.matmul_mx(
+                        out=bank[:, t - t0, :],
+                        lhsT=w2_codes[:, 2 * t * P : 2 * (t + 1) * P].bitcast(FP4X4),
+                        lhsT_scale=w2_scale[:, t * P : (t + 1) * P],
+                        rhs=z_codes[:, cols].bitcast(FP8X4),
+                        rhs_scale=z_scale[:, cols],
+                        start=True,
+                        stop=True,
+                    )
+                nc.scalar.copy(y[c][:, t0 : t0 + per_bank, :], bank[:])
+            nc.sync.dma_start(out_rows[:, :, cols], y[c][:])
+
+        def regroup(c):
+            nc.vector.tensor_copy(
+                y_grouped[c][:].rearrange("p (a i) t -> p a t i", i=4), y[c][:].rearrange("p t (a i) -> p a t i", i=4)
+            )
+
+        def quantize_y(c):
+            cols = slice(c * CHUNK, (c + 1) * CHUNK)
             nc.vector.quantize_mx(
                 out=y_codes[:, cols].bitcast(FP8X4),
                 scales=y_scale[:, cols],
-                in_=y_grouped[:].rearrange("p n t -> p (n t)"),
+                in_=y_grouped[c][:].rearrange("p n t -> p (n t)"),
             )
             if c % 2 == 1:
                 pair = slice((c - 1) * CHUNK, (c + 1) * CHUNK)
                 nc.sync.dma_start(out_words[:, pair], y_codes[:, pair].bitcast(I32))
+
+        center(0, 0, CHUNK)
+        for c in range(1, CHUNKS):
+            center(c, 0, CHUNK // 2)
+            second_layer(c - 1)
+            center(c, CHUNK // 2, CHUNK)
+        regroup(0)
+        second_layer(CHUNKS - 1)
+        quantize_y(0)
+        regroup(1)
+        for c in range(2, CHUNKS):
+            regroup(c)
+            quantize_y(c - 1)
+        quantize_y(CHUNKS - 1)
         for q in range(4):
             queue = nc.scalar if q % 2 == 0 else nc.sync
             queue.dma_start(out_2[0, 4 * q : 4 * q + 4, :].bitcast(I32), y_scale[32 * q : 32 * q + 4, :].bitcast(I32))

@@ -15,16 +15,12 @@ FP8X4 = mybir.dt.float8_e4m3fn_x4
 FP4X4 = mybir.dt.float4_e2m1fn_x4
 ALU = mybir.AluOpType
 COPY = mybir.ActivationFunctionType.Copy
-AXIS_X = mybir.AxisListType.X
 
 P = 128
 PACK = 4
 CHUNK = 128
 CHUNKS = S // CHUNK
-HALF = H // 2
-M_HALF = HALF // PACK
-M_SCALAR = (64, 18)
-GATHERS = ((0, 128), (128, 256), (256, 512))
+M_VECTOR = 84
 
 
 def tile_picked_deepset_none_po_kernel(
@@ -38,118 +34,102 @@ def tile_picked_deepset_none_po_kernel(
         offsets = pool.tile([P, S // 16], U16, name="offsets")
         x_scale_table = pool.tile([P, T], U8, name="x_scale_table", align_bytes=64)
         x_word_table = pool.tile([P, T], U32, name="x_word_table", align_bytes=64)
-        w1_raw = [pool.tile([P, PACK, HALF], F32, name="w1_raw%d" % h, align_bytes=64) for h in range(2)]
+        w1_raw = pool.tile([P, PACK * H], F32, name="w1_raw", align_bytes=64)
+        w2_raw_scales = pool.tile([P, H], U8, name="w2_raw_scales", align_bytes=64)
+        w2_raw = pool.tile([P, 2 * H], U8, name="w2_raw", align_bytes=64)
 
         nc.vector.memset(x_scale_table[:].bitcast(I32), 0)
+        nc.vector.memset(w2_raw_scales[:].bitcast(I32), 0)
+        nc.sync.dma_start(x_word_table[:].bitcast(I32), x_words[0].rearrange("p n r -> p (n r)").bitcast(I32))
         nc.sync.dma_start(offsets[:], offs)
-        w1_rows = w1.rearrange("(p j) c -> p j c", j=PACK)
-        nc.sync.dma_start(w1_raw[0][:], w1_rows[:, :, :HALF])
         for q in range(4):
             nc.sync.dma_start(
                 x_scale_table[32 * q : 32 * q + 4, :].bitcast(I32), x_scales[0, 4 * q : 4 * q + 4, :].bitcast(I32)
             )
-        nc.sync.dma_start(w1_raw[1][:], w1_rows[:, :, HALF:])
-        nc.sync.dma_start(x_word_table[:].bitcast(I32), x_words[0].rearrange("p n r -> p (n r)").bitcast(I32))
-        w2_raw_scales = pool.tile([P, H], U8, name="w2_raw_scales", align_bytes=64)
-        w2_raw = pool.tile([P, 2 * H], U8, name="w2_raw", align_bytes=64)
-        nc.gpsimd.memset(w2_raw_scales[:].bitcast(I32), 0)
+        nc.sync.dma_start(w1_raw[:], w1.rearrange("(p j) c -> p (j c)", j=PACK))
         nc.sync.dma_start(w2_raw[:].bitcast(I32), w2_words[0].bitcast(I32))
         for q in range(4):
             nc.sync.dma_start(
                 w2_raw_scales[32 * q : 32 * q + 4, :].bitcast(I32), w2_scales[0, 4 * q : 4 * q + 4, :].bitcast(I32)
             )
 
-
+        x_codes = pool.tile([P, S], U32, name="x_codes", align_bytes=64)
         x_scale = pool.tile([P, S], U8, name="x_scale", align_bytes=64)
+        nc.vector.tensor_copy(x_codes[:], x_word_table[:].indirect(offsets[:]))
         nc.vector.tensor_copy(x_scale[:], x_scale_table[:].indirect(offsets[:]))
 
-        w1_grouped = pool.tile([P, PACK * H], BF16, name="w1_grouped", align_bytes=64)
-        w1_dst = w1_grouped[:].rearrange("p (t m j) -> p m j t", t=PACK, j=PACK)
-        for h in range(2):
-            src = w1_raw[h][:].rearrange("p j (m t) -> p m j t", t=PACK)
-            m0, cut = h * M_HALF, M_SCALAR[h]
-            nc.scalar.activation(w1_dst[:, m0 : m0 + cut], src[:, :cut], COPY)
-            if cut < M_HALF:
-                nc.vector.tensor_copy(w1_dst[:, m0 + cut : m0 + M_HALF], src[:, cut:])
+        w1_grouped = [pool.tile([P, 2 * P * PACK], BF16, name="w1_grouped%d" % u, align_bytes=64) for u in range(2)]
+        w1_src = w1_raw[:].rearrange("p (j m t) -> p m j t", j=PACK, t=PACK)
+        w1_dst = [g[:].rearrange("p (t m j) -> p m j t", t=2, j=PACK) for g in w1_grouped]
+        nc.vector.tensor_copy(w1_dst[0][:, :M_VECTOR], w1_src[:, :M_VECTOR, :, 0:2])
+        nc.scalar.activation(w1_dst[0][:, M_VECTOR:], w1_src[:, M_VECTOR:, :, 0:2], COPY)
+        nc.scalar.activation(w1_dst[1], w1_src[:, :, :, 2:4], COPY)
         w1_codes = pool.tile([P, H], U32, name="w1_codes", align_bytes=64)
         w1_scale = pool.tile([P, H], U8, name="w1_scale", align_bytes=64)
-        x_codes = pool.tile([P, S], U32, name="x_codes", align_bytes=64)
 
         def quantize_w1(t):
             nc.vector.quantize_mx(
                 out=w1_codes[:, t * P : (t + 1) * P].bitcast(FP8X4),
                 scales=w1_scale[:, t * P : (t + 1) * P],
-                in_=w1_grouped[:, t * PACK * P : (t + 1) * PACK * P],
+                in_=w1_grouped[t // 2][:, (t % 2) * PACK * P : (t % 2 + 1) * PACK * P],
             )
-
-        def gather_words(a, b):
-            nc.vector.tensor_copy(x_codes[:, a:b], x_word_table[:].indirect(offsets[:, a // 16 : b // 16]))
-
-        quantize_w1(0)
-        gather_words(*GATHERS[0])
-        for t in range(1, PACK):
-            quantize_w1(t)
-        for a, b in GATHERS[1:]:
-            gather_words(a, b)
 
         w2_codes = pool.tile([P, 2 * H], U8, name="w2_codes", align_bytes=64)
         w2_scale = pool.tile([P, H], U8, name="w2_scale", align_bytes=64)
+        quantize_w1(0)
+        quantize_w1(1)
         nc.vector.tensor_copy(
             w2_codes[:].rearrange("p (t m b) -> p t m b", t=PACK, b=2),
             w2_raw[:].rearrange("p (m t b) -> p t m b", t=PACK, b=2),
         )
+        quantize_w1(2)
+        quantize_w1(3)
         nc.vector.tensor_copy(
             w2_scale[:].rearrange("p (t m) -> p t m", t=PACK), w2_raw_scales[:].rearrange("p (m t) -> p t m", t=PACK)
         )
 
-        h_banks = [psum.tile([P, PACK, CHUNK], F32, name="h_bank%d" % c) for c in range(CHUNKS)]
-        partial = pool.tile([P, CHUNKS, PACK], F32, name="partial")
-        unread = pool.tile([P, 2, PACK, CHUNK], BF16, name="unread")
-        for c in range(CHUNKS):
-            cols = slice(c * CHUNK, (c + 1) * CHUNK)
-            for t in range(PACK):
-                nc.tensor.matmul_mx(
-                    out=h_banks[c][:, t, :],
-                    lhsT=w1_codes[:, t * P : (t + 1) * P].bitcast(FP8X4),
-                    lhsT_scale=w1_scale[:, t * P : (t + 1) * P],
-                    rhs=x_codes[:, cols].bitcast(FP8X4),
-                    rhs_scale=x_scale[:, cols],
-                    start=True,
-                    stop=True,
-                )
-            if c < 2:
-                for t in range(PACK):
-                    nc.scalar.activation(unread[:, c, t, :], h_banks[c][:, t, :], COPY, accum_out=partial[:, c, t : t + 1])
-            else:
-                nc.vector.tensor_reduce(partial[:, c, :], h_banks[c][:], AXIS_X, ALU.add)
-        total = pool.tile([P, PACK], F32, name="total")
-        nc.vector.tensor_reduce(total[:], partial[:].rearrange("p c t -> p t c"), AXIS_X, ALU.add)
+        mean = [pool.tile([P, 1], F32, name="mean%d" % t) for t in range(PACK)]
+        h_scaled = [pool.tile([P, S], F32, name="h_scaled%d" % t, align_bytes=64) for t in range(PACK)]
+        z = [pool.tile([P, CHUNK * PACK], BF16, name="z%d" % c, align_bytes=64) for c in range(CHUNKS)]
+        z_pairs = pool.tile([P, 2, S - CHUNK, 2], BF16, name="z_pairs", align_bytes=64)
+        for t in range(PACK):
+            bank = psum.tile([P, S], F32, name="h_bank%d" % t)
+            nc.tensor.matmul_mx(
+                out=bank[:],
+                lhsT=w1_codes[:, t * P : (t + 1) * P].bitcast(FP8X4),
+                lhsT_scale=w1_scale[:, t * P : (t + 1) * P],
+                rhs=x_codes[:].bitcast(FP8X4),
+                rhs_scale=x_scale[:],
+                start=True,
+                stop=True,
+            )
+            nc.scalar.activation(h_scaled[t][:], bank[:], COPY, scale=1.0 / S, accum_out=mean[t][:])
+            for dst, cols in (
+                (z[0][:].rearrange("p (n t) -> p n t", t=PACK)[:, :, t], slice(0, CHUNK)),
+                (z_pairs[:, t // 2, :, t % 2], slice(CHUNK, S)),
+            ):
+                nc.vector.tensor_scalar(dst, h_scaled[t][:, cols], float(S), mean[t][:], ALU.mult, ALU.subtract)
 
         z_codes = pool.tile([P, S], U32, name="z_codes", align_bytes=64)
         z_scale = pool.tile([P, S], U8, name="z_scale", align_bytes=64)
         y_codes = pool.tile([P, S], U32, name="y_codes", align_bytes=64)
         y_scale = pool.tile([P, S], U8, name="y_scale", align_bytes=64)
-        z = [pool.tile([P, CHUNK, PACK], BF16, name="z%d" % c, align_bytes=64) for c in range(CHUNKS)]
         y = [pool.tile([P, PACK, CHUNK], F32, name="y%d" % c, align_bytes=64) for c in range(CHUNKS)]
         y_grouped = [pool.tile([P, CHUNK, PACK], BF16, name="y_grouped%d" % c, align_bytes=64) for c in range(CHUNKS)]
         out_rows = out_0.rearrange("(p t) n -> p t n", t=PACK)
         out_words = out_1[0].rearrange("p n r -> p (n r)").bitcast(I32)
 
-        def center(c, a, b):
-            nc.vector.scalar_tensor_tensor(
-                z[c][:, a:b, :],
-                total[:].unsqueeze(1).to_broadcast([P, b - a, PACK]),
-                -1.0 / S,
-                h_banks[c][:, :, a:b].rearrange("p t n -> p n t"),
-                ALU.mult,
-                ALU.add,
+        def merge(c):
+            words = z_pairs[:].rearrange("p u n e -> p u (n e)").bitcast(I32)
+            first = (c - 1) * CHUNK
+            nc.vector.tensor_copy(
+                z[c][:].bitcast(I32).rearrange("p (a i u) -> p a u i", i=4, u=2),
+                words[:, :, first : first + CHUNK].rearrange("p u (a i) -> p a u i", i=4),
             )
 
         def second_layer(c):
             cols = slice(c * CHUNK, (c + 1) * CHUNK)
-            nc.vector.quantize_mx(
-                out=z_codes[:, cols].bitcast(FP8X4), scales=z_scale[:, cols], in_=z[c][:].rearrange("p n t -> p (n t)")
-            )
+            nc.vector.quantize_mx(out=z_codes[:, cols].bitcast(FP8X4), scales=z_scale[:, cols], in_=z[c][:])
             per_bank = PACK // 2 if c == CHUNKS - 1 else PACK
             for t0 in range(0, PACK, per_bank):
                 bank = psum.tile([P, per_bank, CHUNK], F32, name="y_bank", bufs=4)
@@ -182,16 +162,14 @@ def tile_picked_deepset_none_po_kernel(
                 pair = slice((c - 1) * CHUNK, (c + 1) * CHUNK)
                 nc.sync.dma_start(out_words[:, pair], y_codes[:, pair].bitcast(I32))
 
-        center(0, 0, CHUNK)
-        for c in range(1, CHUNKS):
-            center(c, 0, CHUNK // 2)
-            second_layer(c - 1)
-            center(c, CHUNK // 2, CHUNK)
-        regroup(0)
-        second_layer(CHUNKS - 1)
-        quantize_y(0)
-        regroup(1)
+        second_layer(0)
+        merge(1)
         for c in range(2, CHUNKS):
+            merge(c)
+            second_layer(c - 1)
+        second_layer(CHUNKS - 1)
+        regroup(0)
+        for c in range(1, CHUNKS):
             regroup(c)
             quantize_y(c - 1)
         quantize_y(CHUNKS - 1)

@@ -20,7 +20,7 @@ P = 128
 PACK = 4
 CHUNK = 128
 CHUNKS = S // CHUNK
-M_VECTOR = 84
+M_VECTOR = 64
 
 
 def tile_picked_deepset_none_po_kernel(
@@ -93,7 +93,7 @@ def tile_picked_deepset_none_po_kernel(
         z = [pool.tile([P, CHUNK * PACK], BF16, name="z%d" % c, align_bytes=64) for c in range(CHUNKS)]
         z_pairs = pool.tile([P, 2, S - CHUNK, 2], BF16, name="z_pairs", align_bytes=64)
         for t in range(PACK):
-            bank = psum.tile([P, S], F32, name="h_bank%d" % t)
+            bank = psum.tile([P, S], F32, name="bank", bufs=8)
             nc.tensor.matmul_mx(
                 out=bank[:],
                 lhsT=w1_codes[:, t * P : (t + 1) * P].bitcast(FP8X4),
@@ -114,7 +114,9 @@ def tile_picked_deepset_none_po_kernel(
         z_scale = pool.tile([P, S], U8, name="z_scale", align_bytes=64)
         y_codes = pool.tile([P, S], U32, name="y_codes", align_bytes=64)
         y_scale = pool.tile([P, S], U8, name="y_scale", align_bytes=64)
-        y = [pool.tile([P, PACK, CHUNK], F32, name="y%d" % c, align_bytes=64) for c in range(CHUNKS)]
+        y_first = [pool.tile([P, PACK, CHUNK], F32, name="y%d" % c, align_bytes=64) for c in range(2)]
+        y_last = pool.tile([P, PACK, 2 * CHUNK], F32, name="y_last", align_bytes=64)
+        y = [y_first[0][:], y_first[1][:], y_last[:, :, :CHUNK], y_last[:, :, CHUNK:]]
         y_grouped = [pool.tile([P, CHUNK, PACK], BF16, name="y_grouped%d" % c, align_bytes=64) for c in range(CHUNKS)]
         out_rows = out_0.rearrange("(p t) n -> p t n", t=PACK)
         out_words = out_1[0].rearrange("p n r -> p (n r)").bitcast(I32)
@@ -127,12 +129,15 @@ def tile_picked_deepset_none_po_kernel(
                 words[:, :, first : first + CHUNK].rearrange("p u (a i) -> p a u i", i=4),
             )
 
-        def second_layer(c):
+        def quantize_z(c):
             cols = slice(c * CHUNK, (c + 1) * CHUNK)
             nc.vector.quantize_mx(out=z_codes[:, cols].bitcast(FP8X4), scales=z_scale[:, cols], in_=z[c][:])
-            per_bank = PACK // 2 if c == CHUNKS - 1 else PACK
+
+        def second_layer(c):
+            cols = slice(c * CHUNK, (c + 1) * CHUNK)
+            per_bank = PACK if c == 2 else PACK // 2
             for t0 in range(0, PACK, per_bank):
-                bank = psum.tile([P, per_bank, CHUNK], F32, name="y_bank", bufs=4)
+                bank = psum.tile([P, per_bank, CHUNK], F32, name="bank", bufs=8)
                 for t in range(t0, t0 + per_bank):
                     nc.tensor.matmul_mx(
                         out=bank[:, t - t0, :],
@@ -143,12 +148,21 @@ def tile_picked_deepset_none_po_kernel(
                         start=True,
                         stop=True,
                     )
-                nc.scalar.copy(y[c][:, t0 : t0 + per_bank, :], bank[:])
-            nc.sync.dma_start(out_rows[:, :, cols], y[c][:])
+                if c == 2:
+                    nc.vector.tensor_copy(y[c][:, t0 : t0 + per_bank, :], bank[:])
+                else:
+                    nc.scalar.copy(y[c][:, t0 : t0 + per_bank, :], bank[:])
+                if c == 0:
+                    nc.sync.dma_start(out_rows[:, t0 : t0 + per_bank, cols], y[c][:, t0 : t0 + per_bank, :])
+            if c == 1:
+                nc.sync.dma_start(out_rows[:, :, cols], y[c])
+            if c == CHUNKS - 1:
+                nc.sync.dma_start(out_rows[:, :, 2 * CHUNK :], y_last[:])
 
         def regroup(c):
-            nc.vector.tensor_copy(
-                y_grouped[c][:].rearrange("p (a i) t -> p a t i", i=4), y[c][:].rearrange("p t (a i) -> p a t i", i=4)
+            copy = nc.scalar.copy if c == 2 else nc.vector.tensor_copy
+            copy(
+                y_grouped[c][:].rearrange("p (a i) t -> p a t i", i=4), y[c].rearrange("p t (a i) -> p a t i", i=4)
             )
 
         def quantize_y(c):
@@ -158,21 +172,28 @@ def tile_picked_deepset_none_po_kernel(
                 scales=y_scale[:, cols],
                 in_=y_grouped[c][:].rearrange("p n t -> p (n t)"),
             )
-            if c % 2 == 1:
-                pair = slice((c - 1) * CHUNK, (c + 1) * CHUNK)
-                nc.sync.dma_start(out_words[:, pair], y_codes[:, pair].bitcast(I32))
 
+        quantize_z(0)
         second_layer(0)
         merge(1)
-        for c in range(2, CHUNKS):
-            merge(c)
-            second_layer(c - 1)
-        second_layer(CHUNKS - 1)
+        merge(2)
+        quantize_z(1)
+        second_layer(1)
+        merge(3)
+        quantize_z(2)
+        quantize_z(3)
         regroup(0)
-        for c in range(1, CHUNKS):
-            regroup(c)
-            quantize_y(c - 1)
-        quantize_y(CHUNKS - 1)
+        second_layer(2)
+        second_layer(3)
+        quantize_y(0)
+        regroup(1)
+        regroup(2)
+        regroup(3)
+        quantize_y(1)
+        nc.sync.dma_start(out_words[:, : S // 2], y_codes[:, : S // 2].bitcast(I32))
+        quantize_y(3)
+        quantize_y(2)
+        nc.sync.dma_start(out_words[:, S // 2 :], y_codes[:, S // 2 :].bitcast(I32))
         for q in range(4):
             queue = nc.scalar if q % 2 == 0 else nc.sync
             queue.dma_start(out_2[0, 4 * q : 4 * q + 4, :].bitcast(I32), y_scale[32 * q : 32 * q + 4, :].bitcast(I32))

@@ -18,9 +18,13 @@ COPY = mybir.ActivationFunctionType.Copy
 
 P = 128
 PACK = 4
+PAIR = 2
+QUADRANTS = 4
 CHUNK = 128
 CHUNKS = S // CHUNK
-M_VECTOR = 64
+BANKS = 8
+RUN = 4
+M_VECTOR = 52
 
 
 def tile_picked_deepset_none_po_kernel(
@@ -40,50 +44,50 @@ def tile_picked_deepset_none_po_kernel(
 
         nc.vector.memset(x_scale_table[:].bitcast(I32), 0)
         nc.vector.memset(w2_raw_scales[:].bitcast(I32), 0)
+
+        def load_scale_rows(tile, rows):
+            for q in range(QUADRANTS):
+                nc.sync.dma_start(tile[32 * q : 32 * q + 4, :].bitcast(I32), rows[0, 4 * q : 4 * q + 4, :].bitcast(I32))
+
         nc.sync.dma_start(x_word_table[:].bitcast(I32), x_words[0].rearrange("p n r -> p (n r)").bitcast(I32))
         nc.sync.dma_start(offsets[:], offs)
-        for q in range(4):
-            nc.sync.dma_start(
-                x_scale_table[32 * q : 32 * q + 4, :].bitcast(I32), x_scales[0, 4 * q : 4 * q + 4, :].bitcast(I32)
-            )
+        load_scale_rows(x_scale_table, x_scales)
         nc.sync.dma_start(w1_raw[:], w1.rearrange("(p j) c -> p (j c)", j=PACK))
         nc.sync.dma_start(w2_raw[:].bitcast(I32), w2_words[0].bitcast(I32))
-        for q in range(4):
-            nc.sync.dma_start(
-                w2_raw_scales[32 * q : 32 * q + 4, :].bitcast(I32), w2_scales[0, 4 * q : 4 * q + 4, :].bitcast(I32)
-            )
+        load_scale_rows(w2_raw_scales, w2_scales)
 
         x_codes = pool.tile([P, S], U32, name="x_codes", align_bytes=64)
         x_scale = pool.tile([P, S], U8, name="x_scale", align_bytes=64)
         nc.vector.tensor_copy(x_codes[:], x_word_table[:].indirect(offsets[:]))
         nc.vector.tensor_copy(x_scale[:], x_scale_table[:].indirect(offsets[:]))
 
-        w1_grouped = [pool.tile([P, 2 * P * PACK], BF16, name="w1_grouped%d" % u, align_bytes=64) for u in range(2)]
+        w1_grouped = [pool.tile([P, PAIR * P * PACK], BF16, name="w1_grouped%d" % u, align_bytes=64) for u in range(2)]
         w1_src = w1_raw[:].rearrange("p (j m t) -> p m j t", j=PACK, t=PACK)
-        w1_dst = [g[:].rearrange("p (t m j) -> p m j t", t=2, j=PACK) for g in w1_grouped]
-        nc.vector.tensor_copy(w1_dst[0][:, :M_VECTOR], w1_src[:, :M_VECTOR, :, 0:2])
-        nc.scalar.activation(w1_dst[0][:, M_VECTOR:], w1_src[:, M_VECTOR:, :, 0:2], COPY)
-        nc.scalar.activation(w1_dst[1], w1_src[:, :, :, 2:4], COPY)
+        w1_dst = [g[:].rearrange("p (t m j) -> p m j t", t=PAIR, j=PACK) for g in w1_grouped]
+        nc.vector.tensor_copy(w1_dst[0][:, :M_VECTOR], w1_src[:, :M_VECTOR, :, :PAIR])
+        nc.scalar.activation(w1_dst[0][:, M_VECTOR:], w1_src[:, M_VECTOR:, :, :PAIR], COPY)
+        nc.scalar.activation(w1_dst[1], w1_src[:, :, :, PAIR:], COPY)
         w1_codes = pool.tile([P, H], U32, name="w1_codes", align_bytes=64)
         w1_scale = pool.tile([P, H], U8, name="w1_scale", align_bytes=64)
 
         def quantize_w1(t):
+            first = t % PAIR * PACK * P
             nc.vector.quantize_mx(
                 out=w1_codes[:, t * P : (t + 1) * P].bitcast(FP8X4),
                 scales=w1_scale[:, t * P : (t + 1) * P],
-                in_=w1_grouped[t // 2][:, (t % 2) * PACK * P : (t % 2 + 1) * PACK * P],
+                in_=w1_grouped[t // PAIR][:, first : first + PACK * P],
             )
 
         w2_codes = pool.tile([P, 2 * H], U8, name="w2_codes", align_bytes=64)
         w2_scale = pool.tile([P, H], U8, name="w2_scale", align_bytes=64)
-        quantize_w1(0)
-        quantize_w1(1)
+        for t in range(PAIR):
+            quantize_w1(t)
         nc.vector.tensor_copy(
-            w2_codes[:].rearrange("p (t m b) -> p t m b", t=PACK, b=2),
-            w2_raw[:].rearrange("p (m t b) -> p t m b", t=PACK, b=2),
+            w2_codes[:].bitcast(U16).rearrange("p (t m) -> p t m", t=PACK),
+            w2_raw[:].bitcast(U16).rearrange("p (m t) -> p t m", t=PACK),
         )
-        quantize_w1(2)
-        quantize_w1(3)
+        for t in range(PAIR, PACK):
+            quantize_w1(t)
         nc.vector.tensor_copy(
             w2_scale[:].rearrange("p (t m) -> p t m", t=PACK), w2_raw_scales[:].rearrange("p (m t) -> p t m", t=PACK)
         )
@@ -91,11 +95,11 @@ def tile_picked_deepset_none_po_kernel(
         mean = [pool.tile([P, 1], F32, name="mean%d" % t) for t in range(PACK)]
         h_scaled = [pool.tile([P, S], F32, name="h_scaled%d" % t, align_bytes=64) for t in range(PACK)]
         z = [pool.tile([P, CHUNK * PACK], BF16, name="z%d" % c, align_bytes=64) for c in range(CHUNKS)]
-        z_pairs = pool.tile([P, 2, S - CHUNK, 2], BF16, name="z_pairs", align_bytes=64)
+        z_pairs = pool.tile([P, PACK // PAIR, S - CHUNK, PAIR], BF16, name="z_pairs", align_bytes=64)
         for t in range(PACK):
-            bank = psum.tile([P, S], F32, name="bank", bufs=8)
+            h_bank = psum.tile([P, S], F32, name="bank", bufs=BANKS)
             nc.tensor.matmul_mx(
-                out=bank[:],
+                out=h_bank[:],
                 lhsT=w1_codes[:, t * P : (t + 1) * P].bitcast(FP8X4),
                 lhsT_scale=w1_scale[:, t * P : (t + 1) * P],
                 rhs=x_codes[:].bitcast(FP8X4),
@@ -103,10 +107,10 @@ def tile_picked_deepset_none_po_kernel(
                 start=True,
                 stop=True,
             )
-            nc.scalar.activation(h_scaled[t][:], bank[:], COPY, scale=1.0 / S, accum_out=mean[t][:])
+            nc.scalar.activation(h_scaled[t][:], h_bank[:], COPY, scale=1.0 / S, accum_out=mean[t][:])
             for dst, cols in (
                 (z[0][:].rearrange("p (n t) -> p n t", t=PACK)[:, :, t], slice(0, CHUNK)),
-                (z_pairs[:, t // 2, :, t % 2], slice(CHUNK, S)),
+                (z_pairs[:, t // PAIR, :, t % PAIR], slice(CHUNK, S)),
             ):
                 nc.vector.tensor_scalar(dst, h_scaled[t][:, cols], float(S), mean[t][:], ALU.mult, ALU.subtract)
 
@@ -121,48 +125,37 @@ def tile_picked_deepset_none_po_kernel(
         out_rows = out_0.rearrange("(p t) n -> p t n", t=PACK)
         out_words = out_1[0].rearrange("p n r -> p (n r)").bitcast(I32)
 
-        def merge(c):
-            words = z_pairs[:].rearrange("p u n e -> p u (n e)").bitcast(I32)
+        def merge(c, copy):
+            words = z_pairs[:].rearrange("p u n e -> p u (n e)").bitcast(U32)
             first = (c - 1) * CHUNK
-            nc.vector.tensor_copy(
-                z[c][:].bitcast(I32).rearrange("p (a i u) -> p a u i", i=4, u=2),
-                words[:, :, first : first + CHUNK].rearrange("p u (a i) -> p a u i", i=4),
+            copy(
+                z[c][:].bitcast(U32).rearrange("p (a i u) -> p a u i", i=RUN, u=PACK // PAIR),
+                words[:, :, first : first + CHUNK].rearrange("p u (a i) -> p a u i", i=RUN),
             )
 
         def quantize_z(c):
             cols = slice(c * CHUNK, (c + 1) * CHUNK)
             nc.vector.quantize_mx(out=z_codes[:, cols].bitcast(FP8X4), scales=z_scale[:, cols], in_=z[c][:])
 
-        def second_layer(c):
+        def second_layer_pair(c, u, copy):
             cols = slice(c * CHUNK, (c + 1) * CHUNK)
-            per_bank = PACK if c == 2 else PACK // 2
-            for t0 in range(0, PACK, per_bank):
-                bank = psum.tile([P, per_bank, CHUNK], F32, name="bank", bufs=8)
-                for t in range(t0, t0 + per_bank):
-                    nc.tensor.matmul_mx(
-                        out=bank[:, t - t0, :],
-                        lhsT=w2_codes[:, 2 * t * P : 2 * (t + 1) * P].bitcast(FP4X4),
-                        lhsT_scale=w2_scale[:, t * P : (t + 1) * P],
-                        rhs=z_codes[:, cols].bitcast(FP8X4),
-                        rhs_scale=z_scale[:, cols],
-                        start=True,
-                        stop=True,
-                    )
-                if c == 2:
-                    nc.vector.tensor_copy(y[c][:, t0 : t0 + per_bank, :], bank[:])
-                else:
-                    nc.scalar.copy(y[c][:, t0 : t0 + per_bank, :], bank[:])
-                if c == 0:
-                    nc.sync.dma_start(out_rows[:, t0 : t0 + per_bank, cols], y[c][:, t0 : t0 + per_bank, :])
-            if c == 1:
-                nc.sync.dma_start(out_rows[:, :, cols], y[c])
-            if c == CHUNKS - 1:
-                nc.sync.dma_start(out_rows[:, :, 2 * CHUNK :], y_last[:])
+            y_bank = psum.tile([P, PAIR, CHUNK], F32, name="bank", bufs=BANKS)
+            for e in range(PAIR):
+                t = PAIR * u + e
+                nc.tensor.matmul_mx(
+                    out=y_bank[:, e, :],
+                    lhsT=w2_codes[:, 2 * t * P : 2 * (t + 1) * P].bitcast(FP4X4),
+                    lhsT_scale=w2_scale[:, t * P : (t + 1) * P],
+                    rhs=z_codes[:, cols].bitcast(FP8X4),
+                    rhs_scale=z_scale[:, cols],
+                    start=True,
+                    stop=True,
+                )
+            copy(y[c][:, PAIR * u : PAIR * (u + 1), :], y_bank[:])
 
-        def regroup(c):
-            copy = nc.scalar.copy if c == 2 else nc.vector.tensor_copy
+        def regroup(c, copy):
             copy(
-                y_grouped[c][:].rearrange("p (a i) t -> p a t i", i=4), y[c].rearrange("p t (a i) -> p a t i", i=4)
+                y_grouped[c][:].rearrange("p (a i) t -> p a t i", i=RUN), y[c].rearrange("p t (a i) -> p a t i", i=RUN)
             )
 
         def quantize_y(c):
@@ -173,27 +166,34 @@ def tile_picked_deepset_none_po_kernel(
                 in_=y_grouped[c][:].rearrange("p n t -> p (n t)"),
             )
 
+        on_scalar, on_vector = nc.scalar.copy, nc.vector.tensor_copy
+        pairs = [slice(PAIR * u, PAIR * (u + 1)) for u in range(PACK // PAIR)]
+
+        merge(2, on_scalar)
+        merge(3, on_scalar)
         quantize_z(0)
-        second_layer(0)
-        merge(1)
-        merge(2)
-        quantize_z(1)
-        second_layer(1)
-        merge(3)
-        quantize_z(2)
-        quantize_z(3)
-        regroup(0)
-        second_layer(2)
-        second_layer(3)
+        for u, groups in enumerate(pairs):
+            second_layer_pair(0, u, on_scalar)
+            nc.sync.dma_start(out_rows[:, groups, :CHUNK], y[0][:, groups, :])
+        merge(1, on_vector)
+        for c in (2, 1, 3):
+            quantize_z(c)
+        second_layer_pair(1, 0, on_scalar)
+        second_layer_pair(1, 1, on_vector)
+        nc.sync.dma_start(out_rows[:, :, CHUNK : 2 * CHUNK], y[1])
+        regroup(0, on_vector)
+        second_layer_pair(2, 0, on_scalar)
+        second_layer_pair(2, 1, on_vector)
+        for u, groups in enumerate(pairs):
+            second_layer_pair(3, u, on_scalar)
+            nc.sync.dma_start(out_rows[:, groups, 2 * CHUNK :], y_last[:, groups, :])
         quantize_y(0)
-        regroup(1)
-        regroup(2)
-        regroup(3)
-        quantize_y(1)
-        nc.sync.dma_start(out_words[:, : S // 2], y_codes[:, : S // 2].bitcast(I32))
-        quantize_y(3)
-        quantize_y(2)
-        nc.sync.dma_start(out_words[:, S // 2 :], y_codes[:, S // 2 :].bitcast(I32))
-        for q in range(4):
+        regroup(1, on_vector)
+        regroup(2, on_scalar)
+        regroup(3, on_vector)
+        for c in (1, 3, 2):
+            quantize_y(c)
+        nc.sync.dma_start(out_words, y_codes[:].bitcast(I32))
+        for q in range(QUADRANTS):
             queue = nc.scalar if q % 2 == 0 else nc.sync
             queue.dma_start(out_2[0, 4 * q : 4 * q + 4, :].bitcast(I32), y_scale[32 * q : 32 * q + 4, :].bitcast(I32))

@@ -195,5 +195,4 @@ def tile_picked_deepset_none_po_kernel(
             quantize_y(c)
         nc.sync.dma_start(out_words, y_codes[:].bitcast(I32))
         for q in range(QUADRANTS):
-            queue = nc.scalar if q % 2 == 0 else nc.sync
-            queue.dma_start(out_2[0, 4 * q : 4 * q + 4, :].bitcast(I32), y_scale[32 * q : 32 * q + 4, :].bitcast(I32))
+            nc.scalar.dma_start(out_2[0, 4 * q : 4 * q + 4, :].bitcast(I32), y_scale[32 * q : 32 * q + 4, :].bitcast(I32))

@@ -24,7 +24,7 @@ CHUNK = 128
 CHUNKS = S // CHUNK
 BANKS = 8
 RUN = 4
-M_VECTOR = 52
+M_VECTOR = 72
 
 
 def tile_picked_deepset_none_po_kernel(
@@ -118,9 +118,7 @@ def tile_picked_deepset_none_po_kernel(
         z_scale = pool.tile([P, S], U8, name="z_scale", align_bytes=64)
         y_codes = pool.tile([P, S], U32, name="y_codes", align_bytes=64)
         y_scale = pool.tile([P, S], U8, name="y_scale", align_bytes=64)
-        y_first = [pool.tile([P, PACK, CHUNK], F32, name="y%d" % c, align_bytes=64) for c in range(2)]
-        y_last = pool.tile([P, PACK, 2 * CHUNK], F32, name="y_last", align_bytes=64)
-        y = [y_first[0][:], y_first[1][:], y_last[:, :, :CHUNK], y_last[:, :, CHUNK:]]
+        y = [pool.tile([P, PACK, CHUNK], F32, name="y%d" % c, align_bytes=64)[:] for c in range(CHUNKS)]
         y_grouped = [pool.tile([P, CHUNK, PACK], BF16, name="y_grouped%d" % c, align_bytes=64) for c in range(CHUNKS)]
         out_rows = out_0.rearrange("(p t) n -> p t n", t=PACK)
         out_words = out_1[0].rearrange("p n r -> p (n r)").bitcast(I32)
@@ -166,6 +164,9 @@ def tile_picked_deepset_none_po_kernel(
                 in_=y_grouped[c][:].rearrange("p n t -> p (n t)"),
             )
 
+        def store_y(c):
+            nc.sync.dma_start(out_rows[:, :, c * CHUNK : (c + 1) * CHUNK], y[c])
+
         on_scalar, on_vector = nc.scalar.copy, nc.vector.tensor_copy
         pairs = [slice(PAIR * u, PAIR * (u + 1)) for u in range(PACK // PAIR)]
 
@@ -180,13 +181,14 @@ def tile_picked_deepset_none_po_kernel(
             quantize_z(c)
         second_layer_pair(1, 0, on_scalar)
         second_layer_pair(1, 1, on_vector)
-        nc.sync.dma_start(out_rows[:, :, CHUNK : 2 * CHUNK], y[1])
+        store_y(1)
         regroup(0, on_vector)
         second_layer_pair(2, 0, on_scalar)
         second_layer_pair(2, 1, on_vector)
-        for u, groups in enumerate(pairs):
+        store_y(2)
+        for u in range(PACK // PAIR):
             second_layer_pair(3, u, on_scalar)
-            nc.sync.dma_start(out_rows[:, groups, 2 * CHUNK :], y_last[:, groups, :])
+        store_y(3)
         quantize_y(0)
         regroup(1, on_vector)
         regroup(2, on_scalar)

@@ -23,6 +23,7 @@ QUADRANTS = 4
 CHUNK = 128
 CHUNKS = S // CHUNK
 BANKS = 8
+WARM_UP_WIDTHS = (64, 32)
 RUN = 4
 M_VECTOR = 72
 
@@ -96,8 +97,10 @@ def tile_picked_deepset_none_po_kernel(
         h_scaled = [pool.tile([P, S], F32, name="h_scaled%d" % t, align_bytes=64) for t in range(PACK)]
         z = [pool.tile([P, CHUNK * PACK], BF16, name="z%d" % c, align_bytes=64) for c in range(CHUNKS)]
         z_pairs = pool.tile([P, PACK // PAIR, S - CHUNK, PAIR], BF16, name="z_pairs", align_bytes=64)
+        h_banks = []
         for t in range(PACK):
             h_bank = psum.tile([P, S], F32, name="bank", bufs=BANKS)
+            h_banks.append(h_bank)
             nc.tensor.matmul_mx(
                 out=h_bank[:],
                 lhsT=w1_codes[:, t * P : (t + 1) * P].bitcast(FP8X4),
@@ -113,6 +116,17 @@ def tile_picked_deepset_none_po_kernel(
                 (z_pairs[:, t // PAIR, :, t % PAIR], slice(CHUNK, S)),
             ):
                 nc.vector.tensor_scalar(dst, h_scaled[t][:, cols], float(S), mean[t][:], ALU.mult, ALU.subtract)
+
+        for width in WARM_UP_WIDTHS:
+            nc.tensor.matmul_mx(
+                out=h_banks[PACK - 2][:width, :],
+                lhsT=w1_codes[:, :width].bitcast(FP8X4),
+                lhsT_scale=w1_scale[:, :width],
+                rhs=x_codes[:].bitcast(FP8X4),
+                rhs_scale=x_scale[:],
+                start=True,
+                stop=True,
+            )
 
         z_codes = pool.tile([P, S], U32, name="z_codes", align_bytes=64)
         z_scale = pool.tile([P, S], U8, name="z_scale", align_bytes=64)

@@ -20,6 +20,8 @@ P = 128
 PACK = 4
 PAIR = 2
 QUADRANTS = 4
+QUADRANT = P // QUADRANTS
+ROWS = 4
 CHUNK = 128
 CHUNKS = S // CHUNK
 BANKS = 8
@@ -47,8 +49,8 @@ def tile_picked_deepset_none_po_kernel(
         nc.vector.memset(w2_raw_scales[:].bitcast(I32), 0)
 
         def load_scale_rows(tile, rows):
-            for q in range(QUADRANTS):
-                nc.sync.dma_start(tile[32 * q : 32 * q + 4, :].bitcast(I32), rows[0, 4 * q : 4 * q + 4, :].bitcast(I32))
+            for r in range(ROWS):
+                nc.sync.dma_start(tile[r:P:QUADRANT, :].bitcast(I32), rows[0, r : ROWS * QUADRANTS : ROWS, :].bitcast(I32))
 
         nc.sync.dma_start(x_word_table[:].bitcast(I32), x_words[0].rearrange("p n r -> p (n r)").bitcast(I32))
         nc.sync.dma_start(offsets[:], offs)
@@ -97,6 +99,14 @@ def tile_picked_deepset_none_po_kernel(
         h_scaled = [pool.tile([P, S], F32, name="h_scaled%d" % t, align_bytes=64) for t in range(PACK)]
         z = [pool.tile([P, CHUNK * PACK], BF16, name="z%d" % c, align_bytes=64) for c in range(CHUNKS)]
         z_pairs = pool.tile([P, PACK // PAIR, S - CHUNK, PAIR], BF16, name="z_pairs", align_bytes=64)
+
+        def centre(t, first, last):
+            if first == 0:
+                dst = z[0][:].rearrange("p (n t) -> p n t", t=PACK)[:, :, t]
+            else:
+                dst = z_pairs[:, t // PAIR, first - CHUNK : last - CHUNK, t % PAIR]
+            nc.vector.tensor_scalar(dst, h_scaled[t][:, first:last], float(S), mean[t][:], ALU.mult, ALU.subtract)
+
         h_banks = []
         for t in range(PACK):
             h_bank = psum.tile([P, S], F32, name="bank", bufs=BANKS)
@@ -111,11 +121,9 @@ def tile_picked_deepset_none_po_kernel(
                 stop=True,
             )
             nc.scalar.activation(h_scaled[t][:], h_bank[:], COPY, scale=1.0 / S, accum_out=mean[t][:])
-            for dst, cols in (
-                (z[0][:].rearrange("p (n t) -> p n t", t=PACK)[:, :, t], slice(0, CHUNK)),
-                (z_pairs[:, t // PAIR, :, t % PAIR], slice(CHUNK, S)),
-            ):
-                nc.vector.tensor_scalar(dst, h_scaled[t][:, cols], float(S), mean[t][:], ALU.mult, ALU.subtract)
+            if t < PACK - 1:
+                centre(t, 0, CHUNK)
+                centre(t, CHUNK, S)
 
         for width in WARM_UP_WIDTHS:
             nc.tensor.matmul_mx(
@@ -184,14 +192,18 @@ def tile_picked_deepset_none_po_kernel(
         on_scalar, on_vector = nc.scalar.copy, nc.vector.tensor_copy
         pairs = [slice(PAIR * u, PAIR * (u + 1)) for u in range(PACK // PAIR)]
 
-        merge(2, on_scalar)
-        merge(3, on_scalar)
+        centre(PACK - 1, CHUNK, 2 * CHUNK)
+        centre(PACK - 1, 0, CHUNK)
+        merge(1, on_vector)
         quantize_z(0)
+        centre(PACK - 1, 2 * CHUNK, S)
+        merge(2, on_scalar)
         for u, groups in enumerate(pairs):
             second_layer_pair(0, u, on_scalar)
             nc.sync.dma_start(out_rows[:, groups, :CHUNK], y[0][:, groups, :])
-        merge(1, on_vector)
-        for c in (2, 1, 3):
+        quantize_z(1)
+        merge(3, on_vector)
+        for c in (2, 3):
             quantize_z(c)
         second_layer_pair(1, 0, on_scalar)
         second_layer_pair(1, 1, on_vector)
@@ -211,4 +223,5 @@ def tile_picked_deepset_none_po_kernel(
             quantize_y(c)
         nc.sync.dma_start(out_words, y_codes[:].bitcast(I32))
         for q in range(QUADRANTS):
-            nc.scalar.dma_start(out_2[0, 4 * q : 4 * q + 4, :].bitcast(I32), y_scale[32 * q : 32 * q + 4, :].bitcast(I32))
+            live = y_scale[QUADRANT * q : QUADRANT * q + ROWS, :]
+            nc.scalar.dma_start(out_2[0, ROWS * q : ROWS * (q + 1), :].bitcast(I32), live.bitcast(I32))

@@ -15,6 +15,7 @@ FP8X4 = mybir.dt.float8_e4m3fn_x4
 FP4X4 = mybir.dt.float4_e2m1fn_x4
 ALU = mybir.AluOpType
 COPY = mybir.ActivationFunctionType.Copy
+IDENTITY = mybir.ActivationFunctionType.Identity
 
 P = 128
 PACK = 4
@@ -100,12 +101,20 @@ def tile_picked_deepset_none_po_kernel(
         z = [pool.tile([P, CHUNK * PACK], BF16, name="z%d" % c, align_bytes=64) for c in range(CHUNKS)]
         z_pairs = pool.tile([P, PACK // PAIR, S - CHUNK, PAIR], BF16, name="z_pairs", align_bytes=64)
 
-        def centre(t, first, last):
-            if first == 0:
-                dst = z[0][:].rearrange("p (n t) -> p n t", t=PACK)[:, :, t]
-            else:
-                dst = z_pairs[:, t // PAIR, first - CHUNK : last - CHUNK, t % PAIR]
-            nc.vector.tensor_scalar(dst, h_scaled[t][:, first:last], float(S), mean[t][:], ALU.mult, ALU.subtract)
+        def centre_views(t, chunks):
+            src = h_scaled[t][:].rearrange("p (c n) -> p c n", n=CHUNK)[:, chunks]
+            if chunks.start == 0:
+                return z[0][:].rearrange("p (c n t) -> p c n t", c=1, t=PACK)[:, :, :, t], src
+            stored = slice(chunks.start - 1, chunks.stop - 1, chunks.step)
+            return z_pairs[:, t // PAIR, :, t % PAIR].rearrange("p (c n) -> p c n", n=CHUNK)[:, stored], src
+
+        def centre(t, chunks):
+            dst, src = centre_views(t, chunks)
+            nc.vector.tensor_scalar(dst, src, -float(S), mean[t][:], ALU.mult, ALU.add)
+
+        def centre_on_scalar(t, chunks):
+            dst, src = centre_views(t, chunks)
+            nc.scalar.activation(dst, src, IDENTITY, scale=-float(S), bias=mean[t][:])
 
         h_banks = []
         for t in range(PACK):
@@ -120,18 +129,18 @@ def tile_picked_deepset_none_po_kernel(
                 start=True,
                 stop=True,
             )
-            nc.scalar.activation(h_scaled[t][:], h_bank[:], COPY, scale=1.0 / S, accum_out=mean[t][:])
+            nc.scalar.activation(h_scaled[t][:], h_bank[:], COPY, scale=-1.0 / S, accum_out=mean[t][:])
             if t < PACK - 1:
-                centre(t, 0, CHUNK)
-                centre(t, CHUNK, S)
+                centre(t, slice(0, 1))
+                centre(t, slice(1, CHUNKS, 1 if t < PAIR else 2))
 
         for width in WARM_UP_WIDTHS:
             nc.tensor.matmul_mx(
                 out=h_banks[PACK - 2][:width, :],
                 lhsT=w1_codes[:, :width].bitcast(FP8X4),
                 lhsT_scale=w1_scale[:, :width],
-                rhs=x_codes[:].bitcast(FP8X4),
-                rhs_scale=x_scale[:],
+                rhs=w1_codes[:].bitcast(FP8X4),
+                rhs_scale=w1_scale[:],
                 start=True,
                 stop=True,
             )
@@ -192,11 +201,13 @@ def tile_picked_deepset_none_po_kernel(
         on_scalar, on_vector = nc.scalar.copy, nc.vector.tensor_copy
         pairs = [slice(PAIR * u, PAIR * (u + 1)) for u in range(PACK // PAIR)]
 
-        centre(PACK - 1, CHUNK, 2 * CHUNK)
-        centre(PACK - 1, 0, CHUNK)
+        centre(PACK - 1, slice(1, 2))
+        centre(PACK - 1, slice(0, 1))
         merge(1, on_vector)
         quantize_z(0)
-        centre(PACK - 1, 2 * CHUNK, S)
+        centre(PACK - 1, slice(3, 4))
+        for t in range(PAIR, PACK):
+            centre_on_scalar(t, slice(2, 3))
         merge(2, on_scalar)
         for u, groups in enumerate(pairs):
             second_layer_pair(0, u, on_scalar)

@@ -230,9 +230,11 @@ def tile_picked_deepset_none_po_kernel(
         regroup(1, on_vector)
         regroup(2, on_scalar)
         regroup(3, on_vector)
-        for c in (1, 3, 2):
+        quantize_y(1)
+        nc.sync.dma_start(out_words[:, : S // 2], y_codes[:, : S // 2].bitcast(I32))
+        for c in (3, 2):
             quantize_y(c)
-        nc.sync.dma_start(out_words, y_codes[:].bitcast(I32))
+        nc.sync.dma_start(out_words[:, S // 2 :], y_codes[:, S // 2 :].bitcast(I32))
         for q in range(QUADRANTS):
             live = y_scale[QUADRANT * q : QUADRANT * q + ROWS, :]
             nc.scalar.dma_start(out_2[0, ROWS * q : ROWS * (q + 1), :].bitcast(I32), live.bitcast(I32))

@@ -167,10 +167,12 @@ def tile_picked_deepset_none_po_kernel(
             nc.vector.quantize_mx(out=z_codes[:, cols].bitcast(FP8X4), scales=z_scale[:, cols], in_=z[c][:])
 
         def second_layer_pair(c, u, copy):
+            second_layer(c, slice(PAIR * u, PAIR * (u + 1)), copy)
+
+        def second_layer(c, groups, copy):
             cols = slice(c * CHUNK, (c + 1) * CHUNK)
-            y_bank = psum.tile([P, PAIR, CHUNK], F32, name="bank", bufs=BANKS)
-            for e in range(PAIR):
-                t = PAIR * u + e
+            y_bank = psum.tile([P, groups.stop - groups.start, CHUNK], F32, name="bank", bufs=BANKS)
+            for e, t in enumerate(range(groups.start, groups.stop)):
                 nc.tensor.matmul_mx(
                     out=y_bank[:, e, :],
                     lhsT=w2_codes[:, 2 * t * P : 2 * (t + 1) * P].bitcast(FP4X4),
@@ -180,7 +182,7 @@ def tile_picked_deepset_none_po_kernel(
                     start=True,
                     stop=True,
                 )
-            copy(y[c][:, PAIR * u : PAIR * (u + 1), :], y_bank[:])
+            copy(y[c][:, groups, :], y_bank[:])
 
         def regroup(c, copy):
             copy(
@@ -199,7 +201,6 @@ def tile_picked_deepset_none_po_kernel(
             nc.sync.dma_start(out_rows[:, :, c * CHUNK : (c + 1) * CHUNK], y[c])
 
         on_scalar, on_vector = nc.scalar.copy, nc.vector.tensor_copy
-        pairs = [slice(PAIR * u, PAIR * (u + 1)) for u in range(PACK // PAIR)]
 
         centre(PACK - 1, slice(1, 2))
         centre(PACK - 1, slice(0, 1))
@@ -209,8 +210,8 @@ def tile_picked_deepset_none_po_kernel(
         for t in range(PAIR, PACK):
             centre_on_scalar(t, slice(2, 3))
         merge(2, on_scalar)
-        for u, groups in enumerate(pairs):
-            second_layer_pair(0, u, on_scalar)
+        for groups in (slice(0, 1), slice(1, 2), slice(2, 4)):
+            second_layer(0, groups, on_scalar)
             nc.sync.dma_start(out_rows[:, groups, :CHUNK], y[0][:, groups, :])
         quantize_z(1)
         merge(3, on_vector)
@@ -230,11 +231,9 @@ def tile_picked_deepset_none_po_kernel(
         regroup(1, on_vector)
         regroup(2, on_scalar)
         regroup(3, on_vector)
-        quantize_y(1)
-        nc.sync.dma_start(out_words[:, : S // 2], y_codes[:, : S // 2].bitcast(I32))
-        for c in (3, 2):
+        for c in (1, 3, 2):
             quantize_y(c)
-        nc.sync.dma_start(out_words[:, S // 2 :], y_codes[:, S // 2 :].bitcast(I32))
+        nc.sync.dma_start(out_words, y_codes[:].bitcast(I32))
         for q in range(QUADRANTS):
             live = y_scale[QUADRANT * q : QUADRANT * q + ROWS, :]
             nc.scalar.dma_start(out_2[0, ROWS * q : ROWS * (q + 1), :].bitcast(I32), live.bitcast(I32))

@@ -28,7 +28,7 @@ CHUNKS = S // CHUNK
 BANKS = 8
 WARM_UP_WIDTHS = (64, 32)
 RUN = 4
-M_VECTOR = 72
+M_VECTOR = 44
 
 
 def tile_picked_deepset_none_po_kernel(

@@ -28,7 +28,7 @@ CHUNKS = S // CHUNK
 BANKS = 8
 WARM_UP_WIDTHS = (64, 32)
 RUN = 4
-M_VECTOR = 44
+M_VECTOR = 54
 
 
 def tile_picked_deepset_none_po_kernel(

@@ -28,7 +28,8 @@ CHUNKS = S // CHUNK
 BANKS = 8
 WARM_UP_WIDTHS = (64, 32)
 RUN = 4
-M_VECTOR = 54
+M_VECTOR = 84
+STAGE = P - ROWS * QUADRANTS
 
 
 def tile_picked_deepset_none_po_kernel(
@@ -39,31 +40,37 @@ def tile_picked_deepset_none_po_kernel(
         pool = ctx.enter_context(tc.tile_pool(name="sbuf", bufs=1))
         psum = ctx.enter_context(tc.psum_pool(name="psum", bufs=1))
 
+        shared = ctx.enter_context(tc.tile_pool(name="shared", bufs=1))
+
         offsets = pool.tile([P, S // 16], U16, name="offsets")
-        x_scale_table = pool.tile([P, T], U8, name="x_scale_table", align_bytes=64)
         x_word_table = pool.tile([P, T], U32, name="x_word_table", align_bytes=64)
         w1_raw = pool.tile([P, PACK * H], F32, name="w1_raw", align_bytes=64)
-        w2_raw_scales = pool.tile([P, H], U8, name="w2_raw_scales", align_bytes=64)
         w2_raw = pool.tile([P, 2 * H], U8, name="w2_raw", align_bytes=64)
+        x_scale_table = shared.tile([P, T], U8, name="scale_rows", align_bytes=64)
+        x_scale = pool.tile([P, S], U8, name="x_scale", align_bytes=64)
 
-        nc.vector.memset(x_scale_table[:].bitcast(I32), 0)
-        nc.vector.memset(w2_raw_scales[:].bitcast(I32), 0)
+        nc.vector.memset(x_scale_table[:STAGE, :].bitcast(I32), 0)
+        nc.vector.memset(x_scale[:].bitcast(I32), 0)
 
-        def load_scale_rows(tile, rows):
-            for r in range(ROWS):
-                nc.sync.dma_start(tile[r:P:QUADRANT, :].bitcast(I32), rows[0, r : ROWS * QUADRANTS : ROWS, :].bitcast(I32))
-
-        nc.sync.dma_start(x_word_table[:].bitcast(I32), x_words[0].rearrange("p n r -> p (n r)").bitcast(I32))
+        nc.sync.dma_start(x_scale_table[STAGE:, :].bitcast(I32), x_scales[0].bitcast(I32))
         nc.sync.dma_start(offsets[:], offs)
-        load_scale_rows(x_scale_table, x_scales)
+        nc.sync.dma_start(x_word_table[:].bitcast(I32), x_words[0].rearrange("p n r -> p (n r)").bitcast(I32))
         nc.sync.dma_start(w1_raw[:], w1.rearrange("(p j) c -> p (j c)", j=PACK))
         nc.sync.dma_start(w2_raw[:].bitcast(I32), w2_words[0].bitcast(I32))
-        load_scale_rows(w2_raw_scales, w2_scales)
 
         x_codes = pool.tile([P, S], U32, name="x_codes", align_bytes=64)
-        x_scale = pool.tile([P, S], U8, name="x_scale", align_bytes=64)
+        x_scale_picked = pool.tile([P, S], U8, name="x_scale_picked", align_bytes=64)
+        nc.vector.tensor_copy(x_scale_picked[:], x_scale_table[:].indirect(offsets[:]))
+        for r in range(ROWS):
+            nc.sync.dma_start(x_scale[r:P:QUADRANT, :].bitcast(I32), x_scale_picked[STAGE + r : P : ROWS, :].bitcast(I32))
         nc.vector.tensor_copy(x_codes[:], x_word_table[:].indirect(offsets[:]))
-        nc.vector.tensor_copy(x_scale[:], x_scale_table[:].indirect(offsets[:]))
+
+        w2_raw_scales = shared.tile([P, H], U8, name="scale_rows", align_bytes=64)
+        nc.vector.memset(w2_raw_scales[:].bitcast(I32), 0)
+        for r in range(ROWS):
+            nc.sync.dma_start(
+                w2_raw_scales[r:P:QUADRANT, :].bitcast(I32), w2_scales[0, r : ROWS * QUADRANTS : ROWS, :].bitcast(I32)
+            )
 
         w1_grouped = [pool.tile([P, PAIR * P * PACK], BF16, name="w1_grouped%d" % u, align_bytes=64) for u in range(2)]
         w1_src = w1_raw[:].rearrange("p (j m t) -> p m j t", j=PACK, t=PACK)

@@ -45,32 +45,42 @@ def tile_picked_deepset_none_po_kernel(
         offsets = pool.tile([P, S // 16], U16, name="offsets")
         x_word_table = pool.tile([P, T], U32, name="x_word_table", align_bytes=64)
         w1_raw = pool.tile([P, PACK * H], F32, name="w1_raw", align_bytes=64)
-        w2_raw = pool.tile([P, 2 * H], U8, name="w2_raw", align_bytes=64)
+        w2_staged = pool.tile([P, H], U8, name="w2_staged", align_bytes=64)
+        w2_scale = pool.tile([P, H], U8, name="w2_scale", align_bytes=64)
         x_scale_table = shared.tile([P, T], U8, name="scale_rows", align_bytes=64)
         x_scale = pool.tile([P, S], U8, name="x_scale", align_bytes=64)
 
         nc.vector.memset(x_scale_table[:STAGE, :].bitcast(I32), 0)
+        nc.vector.memset(w2_staged[:STAGE, :].bitcast(I32), 0)
         nc.vector.memset(x_scale[:].bitcast(I32), 0)
+        nc.vector.memset(w2_scale[:].bitcast(I32), 0)
 
         nc.sync.dma_start(x_scale_table[STAGE:, :].bitcast(I32), x_scales[0].bitcast(I32))
         nc.sync.dma_start(offsets[:], offs)
         nc.sync.dma_start(x_word_table[:].bitcast(I32), x_words[0].rearrange("p n r -> p (n r)").bitcast(I32))
+        nc.sync.dma_start(w2_staged[STAGE:, :].bitcast(I32), w2_scales[0].bitcast(I32))
         nc.sync.dma_start(w1_raw[:], w1.rearrange("(p j) c -> p (j c)", j=PACK))
-        nc.sync.dma_start(w2_raw[:].bitcast(I32), w2_words[0].bitcast(I32))
 
         x_codes = pool.tile([P, S], U32, name="x_codes", align_bytes=64)
         x_scale_picked = pool.tile([P, S], U8, name="x_scale_picked", align_bytes=64)
         nc.vector.tensor_copy(x_scale_picked[:], x_scale_table[:].indirect(offsets[:]))
-        for r in range(ROWS):
-            nc.sync.dma_start(x_scale[r:P:QUADRANT, :].bitcast(I32), x_scale_picked[STAGE + r : P : ROWS, :].bitcast(I32))
+
+        def place_scale_rows(plane, staged, queues):
+            for r in range(ROWS):
+                queues[r % len(queues)].dma_start(
+                    plane[r:P:QUADRANT, :].bitcast(I32), staged[STAGE + r : P : ROWS, :].bitcast(I32)
+                )
+
+        place_scale_rows(x_scale, x_scale_picked, (nc.sync,))
         nc.vector.tensor_copy(x_codes[:], x_word_table[:].indirect(offsets[:]))
 
-        w2_raw_scales = shared.tile([P, H], U8, name="scale_rows", align_bytes=64)
-        nc.vector.memset(w2_raw_scales[:].bitcast(I32), 0)
-        for r in range(ROWS):
-            nc.sync.dma_start(
-                w2_raw_scales[r:P:QUADRANT, :].bitcast(I32), w2_scales[0, r : ROWS * QUADRANTS : ROWS, :].bitcast(I32)
-            )
+        w2_raw = shared.tile([P, 2 * H], U8, name="scale_rows", align_bytes=64)
+        nc.sync.dma_start(w2_raw[:].bitcast(I32), w2_words[0].bitcast(I32))
+        w2_dealt = pool.tile([P, H], U8, name="w2_dealt", align_bytes=64)
+        nc.vector.tensor_copy(
+            w2_dealt[:].rearrange("p (t m) -> p t m", t=PACK), w2_staged[:].rearrange("p (m t) -> p t m", t=PACK)
+        )
+        place_scale_rows(w2_scale, w2_dealt, (nc.sync,))
 
         w1_grouped = [pool.tile([P, PAIR * P * PACK], BF16, name="w1_grouped%d" % u, align_bytes=64) for u in range(2)]
         w1_src = w1_raw[:].rearrange("p (j m t) -> p m j t", j=PACK, t=PACK)
@@ -90,7 +100,6 @@ def tile_picked_deepset_none_po_kernel(
             )
 
         w2_codes = pool.tile([P, 2 * H], U8, name="w2_codes", align_bytes=64)
-        w2_scale = pool.tile([P, H], U8, name="w2_scale", align_bytes=64)
         for t in range(PAIR):
             quantize_w1(t)
         nc.vector.tensor_copy(
@@ -99,9 +108,6 @@ def tile_picked_deepset_none_po_kernel(
         )
         for t in range(PAIR, PACK):
             quantize_w1(t)
-        nc.vector.tensor_copy(
-            w2_scale[:].rearrange("p (t m) -> p t m", t=PACK), w2_raw_scales[:].rearrange("p (m t) -> p t m", t=PACK)
-        )
 
         mean = [pool.tile([P, 1], F32, name="mean%d" % t) for t in range(PACK)]
         h_scaled = [pool.tile([P, S], F32, name="h_scaled%d" % t, align_bytes=64) for t in range(PACK)]

@@ -44,7 +44,7 @@ def tile_picked_deepset_none_po_kernel(
 
         offsets = pool.tile([P, S // 16], U16, name="offsets")
         x_word_table = pool.tile([P, T], U32, name="x_word_table", align_bytes=64)
-        w1_raw = pool.tile([P, PACK * H], F32, name="w1_raw", align_bytes=64)
+        w1_raw = [pool.tile([P, PAIR * H], F32, name="w1_raw%d" % u, align_bytes=64) for u in range(2)]
         w2_staged = pool.tile([P, H], U8, name="w2_staged", align_bytes=64)
         w2_scale = pool.tile([P, H], U8, name="w2_scale", align_bytes=64)
         x_scale_table = shared.tile([P, T], U8, name="scale_rows", align_bytes=64)
@@ -59,7 +59,9 @@ def tile_picked_deepset_none_po_kernel(
         nc.sync.dma_start(offsets[:], offs)
         nc.sync.dma_start(x_word_table[:].bitcast(I32), x_words[0].rearrange("p n r -> p (n r)").bitcast(I32))
         nc.sync.dma_start(w2_staged[STAGE:, :].bitcast(I32), w2_scales[0].bitcast(I32))
-        nc.sync.dma_start(w1_raw[:], w1.rearrange("(p j) c -> p (j c)", j=PACK))
+        w1_rows = w1.rearrange("(p j) c -> p (j c)", j=PACK)
+        for u in range(2):
+            nc.sync.dma_start(w1_raw[u][:], w1_rows[:, u * PAIR * H : (u + 1) * PAIR * H])
 
         x_codes = pool.tile([P, S], U32, name="x_codes", align_bytes=64)
         x_scale_picked = pool.tile([P, S], U8, name="x_scale_picked", align_bytes=64)
@@ -83,11 +85,14 @@ def tile_picked_deepset_none_po_kernel(
         place_scale_rows(w2_scale, w2_dealt, (nc.sync,))
 
         w1_grouped = [pool.tile([P, PAIR * P * PACK], BF16, name="w1_grouped%d" % u, align_bytes=64) for u in range(2)]
-        w1_src = w1_raw[:].rearrange("p (j m t) -> p m j t", j=PACK, t=PACK)
+        w1_src = [raw[:].rearrange("p (j m t) -> p m j t", j=PAIR, t=PACK) for raw in w1_raw]
         w1_dst = [g[:].rearrange("p (t m j) -> p m j t", t=PAIR, j=PACK) for g in w1_grouped]
-        nc.vector.tensor_copy(w1_dst[0][:, :M_VECTOR], w1_src[:, :M_VECTOR, :, :PAIR])
-        nc.scalar.activation(w1_dst[0][:, M_VECTOR:], w1_src[:, M_VECTOR:, :, :PAIR], COPY)
-        nc.scalar.activation(w1_dst[1], w1_src[:, :, :, PAIR:], COPY)
+        nc.vector.tensor_copy(w1_dst[0][:, :, :PAIR], w1_src[0][:, :, :, :PAIR])
+        nc.scalar.activation(w1_dst[1][:, :, :PAIR], w1_src[0][:, :, :, PAIR:], COPY)
+        for t in range(PAIR):
+            nc.vector.tensor_copy(w1_dst[0][:, :M_VECTOR, PAIR:, t], w1_src[1][:, :M_VECTOR, :, t])
+            nc.scalar.activation(w1_dst[0][:, M_VECTOR:, PAIR:, t], w1_src[1][:, M_VECTOR:, :, t], COPY)
+        nc.scalar.activation(w1_dst[1][:, :, PAIR:], w1_src[1][:, :, :, PAIR:], COPY)
         w1_codes = pool.tile([P, H], U32, name="w1_codes", align_bytes=64)
         w1_scale = pool.tile([P, H], U8, name="w1_scale", align_bytes=64)
 
@@ -162,7 +167,9 @@ def tile_picked_deepset_none_po_kernel(
         z_scale = pool.tile([P, S], U8, name="z_scale", align_bytes=64)
         y_codes = pool.tile([P, S], U32, name="y_codes", align_bytes=64)
         y_scale = pool.tile([P, S], U8, name="y_scale", align_bytes=64)
-        y = [pool.tile([P, PACK, CHUNK], F32, name="y%d" % c, align_bytes=64)[:] for c in range(CHUNKS)]
+        y = [pool.tile([P, PACK, CHUNK], F32, name="y%d" % c, align_bytes=64)[:] for c in range(2)]
+        y_last = pool.tile([P, PACK, 2 * CHUNK], F32, name="y_last", align_bytes=64)
+        y = y + [y_last[:, :, :CHUNK], y_last[:, :, CHUNK:]]
         y_grouped = [pool.tile([P, CHUNK, PACK], BF16, name="y_grouped%d" % c, align_bytes=64) for c in range(CHUNKS)]
         out_rows = out_0.rearrange("(p t) n -> p t n", t=PACK)
         out_words = out_1[0].rearrange("p n r -> p (n r)").bitcast(I32)
@@ -234,12 +241,11 @@ def tile_picked_deepset_none_po_kernel(
         second_layer_pair(1, 1, on_vector)
         store_y(1)
         regroup(0, on_vector)
-        second_layer_pair(2, 0, on_scalar)
-        second_layer_pair(2, 1, on_vector)
-        store_y(2)
-        for u in range(PACK // PAIR):
-            second_layer_pair(3, u, on_scalar)
-        store_y(3)
+        for u, copies in enumerate(((on_scalar, on_vector), (on_scalar, on_scalar))):
+            for c, copy in zip((2, 3), copies):
+                second_layer_pair(c, u, copy)
+            groups = slice(PAIR * u, PAIR * (u + 1))
+            nc.sync.dma_start(out_rows[:, groups, 2 * CHUNK :], y_last[:, groups, :])
         quantize_y(0)
         regroup(1, on_vector)
         regroup(2, on_scalar)

@@ -55,6 +55,11 @@ def tile_picked_deepset_none_po_kernel(
         nc.vector.memset(x_scale[:].bitcast(I32), 0)
         nc.vector.memset(w2_scale[:].bitcast(I32), 0)
 
+        one = pool.tile([P, 1], F32, name="one")
+        minus_s = pool.tile([P, 1], F32, name="minus_s")
+        nc.vector.memset(one[:], 1.0)
+        nc.scalar.activation(minus_s[:], one[:], COPY, scale=-float(S))
+
         nc.sync.dma_start(x_scale_table[STAGE:, :].bitcast(I32), x_scales[0].bitcast(I32))
         nc.sync.dma_start(offsets[:], offs)
         nc.sync.dma_start(x_word_table[:].bitcast(I32), x_words[0].rearrange("p n r -> p (n r)").bitcast(I32))
@@ -73,7 +78,7 @@ def tile_picked_deepset_none_po_kernel(
                     plane[r:P:QUADRANT, :].bitcast(I32), staged[STAGE + r : P : ROWS, :].bitcast(I32)
                 )
 
-        place_scale_rows(x_scale, x_scale_picked, (nc.sync,))
+        place_scale_rows(x_scale, x_scale_picked, (nc.sync, nc.scalar))
         nc.vector.tensor_copy(x_codes[:], x_word_table[:].indirect(offsets[:]))
 
         w2_raw = shared.tile([P, 2 * H], U8, name="scale_rows", align_bytes=64)
@@ -132,7 +137,7 @@ def tile_picked_deepset_none_po_kernel(
 
         def centre_on_scalar(t, chunks):
             dst, src = centre_views(t, chunks)
-            nc.scalar.activation(dst, src, IDENTITY, scale=-float(S), bias=mean[t][:])
+            nc.scalar.activation(dst, src, IDENTITY, scale=minus_s[:], bias=mean[t][:])
 
         h_banks = []
         for t in range(PACK):

@@ -29,6 +29,7 @@ BANKS = 8
 WARM_UP_WIDTHS = (64, 32)
 RUN = 4
 M_VECTOR = 84
+DMA_ALIGN = 256
 STAGE = P - ROWS * QUADRANTS
 
 
@@ -42,13 +43,13 @@ def tile_picked_deepset_none_po_kernel(
 
         shared = ctx.enter_context(tc.tile_pool(name="shared", bufs=1))
 
-        offsets = pool.tile([P, S // 16], U16, name="offsets")
-        x_word_table = pool.tile([P, T], U32, name="x_word_table", align_bytes=64)
-        w1_raw = [pool.tile([P, PAIR * H], F32, name="w1_raw%d" % u, align_bytes=64) for u in range(2)]
-        w2_staged = pool.tile([P, H], U8, name="w2_staged", align_bytes=64)
-        w2_scale = pool.tile([P, H], U8, name="w2_scale", align_bytes=64)
-        x_scale_table = shared.tile([P, T], U8, name="scale_rows", align_bytes=64)
-        x_scale = pool.tile([P, S], U8, name="x_scale", align_bytes=64)
+        offsets = pool.tile([P, S // 16], U16, name="offsets", align_bytes=DMA_ALIGN)
+        x_word_table = pool.tile([P, T], U32, name="x_word_table", align_bytes=DMA_ALIGN)
+        w1_raw = [pool.tile([P, PAIR * H], F32, name="w1_raw%d" % u, align_bytes=DMA_ALIGN) for u in range(2)]
+        w2_staged = pool.tile([P, H], U8, name="w2_staged", align_bytes=DMA_ALIGN)
+        w2_scale = pool.tile([P, H], U8, name="w2_scale", align_bytes=DMA_ALIGN)
+        x_scale_table = shared.tile([P, T], U8, name="scale_rows", align_bytes=DMA_ALIGN)
+        x_scale = pool.tile([P, S], U8, name="x_scale", align_bytes=DMA_ALIGN)
 
         nc.vector.memset(x_scale_table[:STAGE, :].bitcast(I32), 0)
         nc.vector.memset(w2_staged[:STAGE, :].bitcast(I32), 0)
@@ -69,7 +70,7 @@ def tile_picked_deepset_none_po_kernel(
             nc.sync.dma_start(w1_raw[u][:], w1_rows[:, u * PAIR * H : (u + 1) * PAIR * H])
 
         x_codes = pool.tile([P, S], U32, name="x_codes", align_bytes=64)
-        x_scale_picked = pool.tile([P, S], U8, name="x_scale_picked", align_bytes=64)
+        x_scale_picked = pool.tile([P, S], U8, name="x_scale_picked", align_bytes=DMA_ALIGN)
         nc.vector.tensor_copy(x_scale_picked[:], x_scale_table[:].indirect(offsets[:]))
 
         def place_scale_rows(plane, staged, queues):
@@ -81,9 +82,9 @@ def tile_picked_deepset_none_po_kernel(
         place_scale_rows(x_scale, x_scale_picked, (nc.sync, nc.scalar))
         nc.vector.tensor_copy(x_codes[:], x_word_table[:].indirect(offsets[:]))
 
-        w2_raw = shared.tile([P, 2 * H], U8, name="scale_rows", align_bytes=64)
+        w2_raw = shared.tile([P, 2 * H], U8, name="scale_rows", align_bytes=DMA_ALIGN)
         nc.sync.dma_start(w2_raw[:].bitcast(I32), w2_words[0].bitcast(I32))
-        w2_dealt = pool.tile([P, H], U8, name="w2_dealt", align_bytes=64)
+        w2_dealt = pool.tile([P, H], U8, name="w2_dealt", align_bytes=DMA_ALIGN)
         nc.vector.tensor_copy(
             w2_dealt[:].rearrange("p (t m) -> p t m", t=PACK), w2_staged[:].rearrange("p (m t) -> p t m", t=PACK)
         )
@@ -170,10 +171,10 @@ def tile_picked_deepset_none_po_kernel(
 
         z_codes = pool.tile([P, S], U32, name="z_codes", align_bytes=64)
         z_scale = pool.tile([P, S], U8, name="z_scale", align_bytes=64)
-        y_codes = pool.tile([P, S], U32, name="y_codes", align_bytes=64)
-        y_scale = pool.tile([P, S], U8, name="y_scale", align_bytes=64)
-        y = [pool.tile([P, PACK, CHUNK], F32, name="y%d" % c, align_bytes=64)[:] for c in range(2)]
-        y_last = pool.tile([P, PACK, 2 * CHUNK], F32, name="y_last", align_bytes=64)
+        y_codes = pool.tile([P, S], U32, name="y_codes", align_bytes=DMA_ALIGN)
+        y_scale = pool.tile([P, S], U8, name="y_scale", align_bytes=DMA_ALIGN)
+        y = [pool.tile([P, PACK, CHUNK], F32, name="y%d" % c, align_bytes=DMA_ALIGN)[:] for c in range(2)]
+        y_last = pool.tile([P, PACK, 2 * CHUNK], F32, name="y_last", align_bytes=DMA_ALIGN)
         y = y + [y_last[:, :, :CHUNK], y_last[:, :, CHUNK:]]
         y_grouped = [pool.tile([P, CHUNK, PACK], BF16, name="y_grouped%d" % c, align_bytes=64) for c in range(CHUNKS)]
         out_rows = out_0.rearrange("(p t) n -> p t n", t=PACK)

@@ -29,7 +29,7 @@ BANKS = 8
 WARM_UP_WIDTHS = (64, 32)
 RUN = 4
 M_VECTOR = 84
-DMA_ALIGN = 256
+ALIGN = 256
 STAGE = P - ROWS * QUADRANTS
 
 
@@ -43,13 +43,13 @@ def tile_picked_deepset_none_po_kernel(
 
         shared = ctx.enter_context(tc.tile_pool(name="shared", bufs=1))
 
-        offsets = pool.tile([P, S // 16], U16, name="offsets", align_bytes=DMA_ALIGN)
-        x_word_table = pool.tile([P, T], U32, name="x_word_table", align_bytes=DMA_ALIGN)
-        w1_raw = [pool.tile([P, PAIR * H], F32, name="w1_raw%d" % u, align_bytes=DMA_ALIGN) for u in range(2)]
-        w2_staged = pool.tile([P, H], U8, name="w2_staged", align_bytes=DMA_ALIGN)
-        w2_scale = pool.tile([P, H], U8, name="w2_scale", align_bytes=DMA_ALIGN)
-        x_scale_table = shared.tile([P, T], U8, name="scale_rows", align_bytes=DMA_ALIGN)
-        x_scale = pool.tile([P, S], U8, name="x_scale", align_bytes=DMA_ALIGN)
+        offsets = pool.tile([P, S // 16], U16, name="offsets", align_bytes=ALIGN)
+        x_word_table = pool.tile([P, T], U32, name="x_word_table", align_bytes=ALIGN)
+        w1_raw = [pool.tile([P, PAIR * H], F32, name="w1_raw%d" % u, align_bytes=ALIGN) for u in range(2)]
+        w2_staged = pool.tile([P, H], U8, name="w2_staged", align_bytes=ALIGN)
+        w2_scale = pool.tile([P, H], U8, name="w2_scale", align_bytes=ALIGN)
+        x_scale_table = shared.tile([P, T], U8, name="scale_rows", align_bytes=ALIGN)
+        x_scale = pool.tile([P, S], U8, name="x_scale", align_bytes=ALIGN)
 
         nc.vector.memset(x_scale_table[:STAGE, :].bitcast(I32), 0)
         nc.vector.memset(w2_staged[:STAGE, :].bitcast(I32), 0)
@@ -69,8 +69,8 @@ def tile_picked_deepset_none_po_kernel(
         for u in range(2):
             nc.sync.dma_start(w1_raw[u][:], w1_rows[:, u * PAIR * H : (u + 1) * PAIR * H])
 
-        x_codes = pool.tile([P, S], U32, name="x_codes", align_bytes=64)
-        x_scale_picked = pool.tile([P, S], U8, name="x_scale_picked", align_bytes=DMA_ALIGN)
+        x_codes = pool.tile([P, S], U32, name="x_codes", align_bytes=ALIGN)
+        x_scale_picked = pool.tile([P, S], U8, name="x_scale_picked", align_bytes=ALIGN)
         nc.vector.tensor_copy(x_scale_picked[:], x_scale_table[:].indirect(offsets[:]))
 
         def place_scale_rows(plane, staged, queues):
@@ -82,15 +82,15 @@ def tile_picked_deepset_none_po_kernel(
         place_scale_rows(x_scale, x_scale_picked, (nc.sync, nc.scalar))
         nc.vector.tensor_copy(x_codes[:], x_word_table[:].indirect(offsets[:]))
 
-        w2_raw = shared.tile([P, 2 * H], U8, name="scale_rows", align_bytes=DMA_ALIGN)
+        w2_raw = shared.tile([P, 2 * H], U8, name="scale_rows", align_bytes=ALIGN)
         nc.sync.dma_start(w2_raw[:].bitcast(I32), w2_words[0].bitcast(I32))
-        w2_dealt = pool.tile([P, H], U8, name="w2_dealt", align_bytes=DMA_ALIGN)
+        w2_dealt = pool.tile([P, H], U8, name="w2_dealt", align_bytes=ALIGN)
         nc.vector.tensor_copy(
             w2_dealt[:].rearrange("p (t m) -> p t m", t=PACK), w2_staged[:].rearrange("p (m t) -> p t m", t=PACK)
         )
         place_scale_rows(w2_scale, w2_dealt, (nc.sync,))
 
-        w1_grouped = [pool.tile([P, PAIR * P * PACK], BF16, name="w1_grouped%d" % u, align_bytes=64) for u in range(2)]
+        w1_grouped = [pool.tile([P, PAIR * P * PACK], BF16, name="w1_grouped%d" % u, align_bytes=ALIGN) for u in range(2)]
         w1_src = [raw[:].rearrange("p (j m t) -> p m j t", j=PAIR, t=PACK) for raw in w1_raw]
         w1_dst = [g[:].rearrange("p (t m j) -> p m j t", t=PAIR, j=PACK) for g in w1_grouped]
         nc.vector.tensor_copy(w1_dst[0][:, :, :PAIR], w1_src[0][:, :, :, :PAIR])
@@ -99,8 +99,8 @@ def tile_picked_deepset_none_po_kernel(
             nc.vector.tensor_copy(w1_dst[0][:, :M_VECTOR, PAIR:, t], w1_src[1][:, :M_VECTOR, :, t])
             nc.scalar.activation(w1_dst[0][:, M_VECTOR:, PAIR:, t], w1_src[1][:, M_VECTOR:, :, t], COPY)
         nc.scalar.activation(w1_dst[1][:, :, PAIR:], w1_src[1][:, :, :, PAIR:], COPY)
-        w1_codes = pool.tile([P, H], U32, name="w1_codes", align_bytes=64)
-        w1_scale = pool.tile([P, H], U8, name="w1_scale", align_bytes=64)
+        w1_codes = pool.tile([P, H], U32, name="w1_codes", align_bytes=ALIGN)
+        w1_scale = pool.tile([P, H], U8, name="w1_scale", align_bytes=ALIGN)
 
         def quantize_w1(t):
             first = t % PAIR * PACK * P
@@ -110,7 +110,7 @@ def tile_picked_deepset_none_po_kernel(
                 in_=w1_grouped[t // PAIR][:, first : first + PACK * P],
             )
 
-        w2_codes = pool.tile([P, 2 * H], U8, name="w2_codes", align_bytes=64)
+        w2_codes = pool.tile([P, 2 * H], U8, name="w2_codes", align_bytes=ALIGN)
         for t in range(PAIR):
             quantize_w1(t)
         nc.vector.tensor_copy(
@@ -121,9 +121,9 @@ def tile_picked_deepset_none_po_kernel(
             quantize_w1(t)
 
         mean = [pool.tile([P, 1], F32, name="mean%d" % t) for t in range(PACK)]
-        h_scaled = [pool.tile([P, S], F32, name="h_scaled%d" % t, align_bytes=64) for t in range(PACK)]
-        z = [pool.tile([P, CHUNK * PACK], BF16, name="z%d" % c, align_bytes=64) for c in range(CHUNKS)]
-        z_pairs = pool.tile([P, PACK // PAIR, S - CHUNK, PAIR], BF16, name="z_pairs", align_bytes=64)
+        h_scaled = [pool.tile([P, S], F32, name="h_scaled%d" % t, align_bytes=ALIGN) for t in range(PACK)]
+        z = [pool.tile([P, CHUNK * PACK], BF16, name="z%d" % c, align_bytes=ALIGN) for c in range(CHUNKS)]
+        z_pairs = pool.tile([P, PACK // PAIR, S - CHUNK, PAIR], BF16, name="z_pairs", align_bytes=ALIGN)
 
         def centre_views(t, chunks):
             src = h_scaled[t][:].rearrange("p (c n) -> p c n", n=CHUNK)[:, chunks]
@@ -169,14 +169,14 @@ def tile_picked_deepset_none_po_kernel(
                 stop=True,
             )
 
-        z_codes = pool.tile([P, S], U32, name="z_codes", align_bytes=64)
-        z_scale = pool.tile([P, S], U8, name="z_scale", align_bytes=64)
-        y_codes = pool.tile([P, S], U32, name="y_codes", align_bytes=DMA_ALIGN)
-        y_scale = pool.tile([P, S], U8, name="y_scale", align_bytes=DMA_ALIGN)
-        y = [pool.tile([P, PACK, CHUNK], F32, name="y%d" % c, align_bytes=DMA_ALIGN)[:] for c in range(2)]
-        y_last = pool.tile([P, PACK, 2 * CHUNK], F32, name="y_last", align_bytes=DMA_ALIGN)
+        z_codes = pool.tile([P, S], U32, name="z_codes", align_bytes=ALIGN)
+        z_scale = pool.tile([P, S], U8, name="z_scale", align_bytes=ALIGN)
+        y_codes = pool.tile([P, S], U32, name="y_codes", align_bytes=ALIGN)
+        y_scale = pool.tile([P, S], U8, name="y_scale", align_bytes=ALIGN)
+        y = [pool.tile([P, PACK, CHUNK], F32, name="y%d" % c, align_bytes=ALIGN)[:] for c in range(2)]
+        y_last = pool.tile([P, PACK, 2 * CHUNK], F32, name="y_last", align_bytes=ALIGN)
         y = y + [y_last[:, :, :CHUNK], y_last[:, :, CHUNK:]]
-        y_grouped = [pool.tile([P, CHUNK, PACK], BF16, name="y_grouped%d" % c, align_bytes=64) for c in range(CHUNKS)]
+        y_grouped = [pool.tile([P, CHUNK, PACK], BF16, name="y_grouped%d" % c, align_bytes=ALIGN) for c in range(CHUNKS)]
         out_rows = out_0.rearrange("(p t) n -> p t n", t=PACK)
         out_words = out_1[0].rearrange("p n r -> p (n r)").bitcast(I32)
 

@@ -79,7 +79,7 @@ def tile_picked_deepset_none_po_kernel(
                     plane[r:P:QUADRANT, :].bitcast(I32), staged[STAGE + r : P : ROWS, :].bitcast(I32)
                 )
 
-        place_scale_rows(x_scale, x_scale_picked, (nc.sync, nc.scalar))
+        place_scale_rows(x_scale, x_scale_picked, (nc.scalar, nc.sync, nc.scalar, nc.scalar))
         nc.vector.tensor_copy(x_codes[:], x_word_table[:].indirect(offsets[:]))
 
         w2_raw = shared.tile([P, 2 * H], U8, name="scale_rows", align_bytes=ALIGN)

from contextlib import ExitStack

import concourse.mybir as mybir

K, T, S, H = 512, 1024, 512, 512
FLOPS = 2 * K * H * S + 2 * H * H * S

F32 = mybir.dt.float32
BF16 = mybir.dt.bfloat16
I32 = mybir.dt.int32
U32 = mybir.dt.uint32
U16 = mybir.dt.uint16
U8 = mybir.dt.uint8
FP8X4 = mybir.dt.float8_e4m3fn_x4
FP4X4 = mybir.dt.float4_e2m1fn_x4
ALU = mybir.AluOpType
COPY = mybir.ActivationFunctionType.Copy
IDENTITY = mybir.ActivationFunctionType.Identity

P = 128
PACK = 4
PAIR = 2
QUADRANTS = 4
QUADRANT = P // QUADRANTS
ROWS = 4
CHUNK = 128
CHUNKS = S // CHUNK
BANKS = 8
WARM_UP_WIDTHS = (64, 32)
RUN = 4
M_VECTOR = 84
ALIGN = 256
STAGE = P - ROWS * QUADRANTS


def tile_picked_deepset_none_po_kernel(
    tc, x_words, x_scales, w1, w2_words, w2_scales, offs, out_0, out_1, out_2
):
    nc = tc.nc
    with ExitStack() as ctx:
        pool = ctx.enter_context(tc.tile_pool(name="sbuf", bufs=1))
        psum = ctx.enter_context(tc.psum_pool(name="psum", bufs=1))

        shared = ctx.enter_context(tc.tile_pool(name="shared", bufs=1))

        offsets = pool.tile([P, S // 16], U16, name="offsets", align_bytes=ALIGN)
        x_word_table = pool.tile([P, T], U32, name="x_word_table", align_bytes=ALIGN)
        w1_raw = [pool.tile([P, PAIR * H], F32, name="w1_raw%d" % u, align_bytes=ALIGN) for u in range(2)]
        w2_staged = pool.tile([P, H], U8, name="w2_staged", align_bytes=ALIGN)
        w2_scale = pool.tile([P, H], U8, name="w2_scale", align_bytes=ALIGN)
        x_scale_table = shared.tile([P, T], U8, name="scale_rows", align_bytes=ALIGN)
        x_scale = pool.tile([P, S], U8, name="x_scale", align_bytes=ALIGN)

        nc.vector.memset(x_scale_table[:STAGE, :].bitcast(I32), 0)
        nc.vector.memset(w2_staged[:STAGE, :].bitcast(I32), 0)
        nc.vector.memset(x_scale[:].bitcast(I32), 0)
        nc.vector.memset(w2_scale[:].bitcast(I32), 0)

        one = pool.tile([P, 1], F32, name="one")
        minus_s = pool.tile([P, 1], F32, name="minus_s")
        nc.vector.memset(one[:], 1.0)
        nc.scalar.activation(minus_s[:], one[:], COPY, scale=-float(S))

        nc.sync.dma_start(x_scale_table[STAGE:, :].bitcast(I32), x_scales[0].bitcast(I32))
        nc.sync.dma_start(offsets[:], offs)
        nc.sync.dma_start(x_word_table[:].bitcast(I32), x_words[0].rearrange("p n r -> p (n r)").bitcast(I32))
        nc.sync.dma_start(w2_staged[STAGE:, :].bitcast(I32), w2_scales[0].bitcast(I32))
        w1_rows = w1.rearrange("(p j) c -> p (j c)", j=PACK)
        for u in range(2):
            nc.sync.dma_start(w1_raw[u][:], w1_rows[:, u * PAIR * H : (u + 1) * PAIR * H])

        x_codes = pool.tile([P, S], U32, name="x_codes", align_bytes=ALIGN)
        x_scale_picked = pool.tile([P, S], U8, name="x_scale_picked", align_bytes=ALIGN)
        nc.vector.tensor_copy(x_scale_picked[:], x_scale_table[:].indirect(offsets[:]))

        def place_scale_rows(plane, staged, queues):
            for r in range(ROWS):
                queues[r % len(queues)].dma_start(
                    plane[r:P:QUADRANT, :].bitcast(I32), staged[STAGE + r : P : ROWS, :].bitcast(I32)
                )

        place_scale_rows(x_scale, x_scale_picked, (nc.scalar, nc.sync, nc.scalar, nc.scalar))
        nc.vector.tensor_copy(x_codes[:], x_word_table[:].indirect(offsets[:]))

        w2_raw = shared.tile([P, 2 * H], U8, name="scale_rows", align_bytes=ALIGN)
        nc.sync.dma_start(w2_raw[:].bitcast(I32), w2_words[0].bitcast(I32))
        w2_dealt = pool.tile([P, H], U8, name="w2_dealt", align_bytes=ALIGN)
        nc.vector.tensor_copy(
            w2_dealt[:].rearrange("p (t m) -> p t m", t=PACK), w2_staged[:].rearrange("p (m t) -> p t m", t=PACK)
        )
        place_scale_rows(w2_scale, w2_dealt, (nc.sync,))

        w1_grouped = [pool.tile([P, PAIR * P * PACK], BF16, name="w1_grouped%d" % u, align_bytes=ALIGN) for u in range(2)]
        w1_src = [raw[:].rearrange("p (j m t) -> p m j t", j=PAIR, t=PACK) for raw in w1_raw]
        w1_dst = [g[:].rearrange("p (t m j) -> p m j t", t=PAIR, j=PACK) for g in w1_grouped]
        nc.vector.tensor_copy(w1_dst[0][:, :, :PAIR], w1_src[0][:, :, :, :PAIR])
        nc.scalar.activation(w1_dst[1][:, :, :PAIR], w1_src[0][:, :, :, PAIR:], COPY)
        for t in range(PAIR):
            nc.vector.tensor_copy(w1_dst[0][:, :M_VECTOR, PAIR:, t], w1_src[1][:, :M_VECTOR, :, t])
            nc.scalar.activation(w1_dst[0][:, M_VECTOR:, PAIR:, t], w1_src[1][:, M_VECTOR:, :, t], COPY)
        nc.scalar.activation(w1_dst[1][:, :, PAIR:], w1_src[1][:, :, :, PAIR:], COPY)
        w1_codes = pool.tile([P, H], U32, name="w1_codes", align_bytes=ALIGN)
        w1_scale = pool.tile([P, H], U8, name="w1_scale", align_bytes=ALIGN)

        def quantize_w1(t):
            first = t % PAIR * PACK * P
            nc.vector.quantize_mx(
                out=w1_codes[:, t * P : (t + 1) * P].bitcast(FP8X4),
                scales=w1_scale[:, t * P : (t + 1) * P],
                in_=w1_grouped[t // PAIR][:, first : first + PACK * P],
            )

        w2_codes = pool.tile([P, 2 * H], U8, name="w2_codes", align_bytes=ALIGN)
        for t in range(PAIR):
            quantize_w1(t)
        nc.vector.tensor_copy(
            w2_codes[:].bitcast(U16).rearrange("p (t m) -> p t m", t=PACK),
            w2_raw[:].bitcast(U16).rearrange("p (m t) -> p t m", t=PACK),
        )
        for t in range(PAIR, PACK):
            quantize_w1(t)

        mean = [pool.tile([P, 1], F32, name="mean%d" % t) for t in range(PACK)]
        h_scaled = [pool.tile([P, S], F32, name="h_scaled%d" % t, align_bytes=ALIGN) for t in range(PACK)]
        z = [pool.tile([P, CHUNK * PACK], BF16, name="z%d" % c, align_bytes=ALIGN) for c in range(CHUNKS)]
        z_pairs = pool.tile([P, PACK // PAIR, S - CHUNK, PAIR], BF16, name="z_pairs", align_bytes=ALIGN)

        def centre_views(t, chunks):
            src = h_scaled[t][:].rearrange("p (c n) -> p c n", n=CHUNK)[:, chunks]
            if chunks.start == 0:
                return z[0][:].rearrange("p (c n t) -> p c n t", c=1, t=PACK)[:, :, :, t], src
            stored = slice(chunks.start - 1, chunks.stop - 1, chunks.step)
            return z_pairs[:, t // PAIR, :, t % PAIR].rearrange("p (c n) -> p c n", n=CHUNK)[:, stored], src

        def centre(t, chunks):
            dst, src = centre_views(t, chunks)
            nc.vector.tensor_scalar(dst, src, -float(S), mean[t][:], ALU.mult, ALU.add)

        def centre_on_scalar(t, chunks):
            dst, src = centre_views(t, chunks)
            nc.scalar.activation(dst, src, IDENTITY, scale=minus_s[:], bias=mean[t][:])

        h_banks = []
        for t in range(PACK):
            h_bank = psum.tile([P, S], F32, name="bank", bufs=BANKS)
            h_banks.append(h_bank)
            nc.tensor.matmul_mx(
                out=h_bank[:],
                lhsT=w1_codes[:, t * P : (t + 1) * P].bitcast(FP8X4),
                lhsT_scale=w1_scale[:, t * P : (t + 1) * P],
                rhs=x_codes[:].bitcast(FP8X4),
                rhs_scale=x_scale[:],
                start=True,
                stop=True,
            )
            nc.scalar.activation(h_scaled[t][:], h_bank[:], COPY, scale=-1.0 / S, accum_out=mean[t][:])
            if t < PACK - 1:
                centre(t, slice(0, 1))
                centre(t, slice(1, CHUNKS, 1 if t < PAIR else 2))

        for width in WARM_UP_WIDTHS:
            nc.tensor.matmul_mx(
                out=h_banks[PACK - 2][:width, :],
                lhsT=w1_codes[:, :width].bitcast(FP8X4),
                lhsT_scale=w1_scale[:, :width],
                rhs=w1_codes[:].bitcast(FP8X4),
                rhs_scale=w1_scale[:],
                start=True,
                stop=True,
            )

        z_codes = pool.tile([P, S], U32, name="z_codes", align_bytes=ALIGN)
        z_scale = pool.tile([P, S], U8, name="z_scale", align_bytes=ALIGN)
        y_codes = pool.tile([P, S], U32, name="y_codes", align_bytes=ALIGN)
        y_scale = pool.tile([P, S], U8, name="y_scale", align_bytes=ALIGN)
        y = [pool.tile([P, PACK, CHUNK], F32, name="y%d" % c, align_bytes=ALIGN)[:] for c in range(2)]
        y_last = pool.tile([P, PACK, 2 * CHUNK], F32, name="y_last", align_bytes=ALIGN)
        y = y + [y_last[:, :, :CHUNK], y_last[:, :, CHUNK:]]
        y_grouped = [pool.tile([P, CHUNK, PACK], BF16, name="y_grouped%d" % c, align_bytes=ALIGN) for c in range(CHUNKS)]
        out_rows = out_0.rearrange("(p t) n -> p t n", t=PACK)
        out_words = out_1[0].rearrange("p n r -> p (n r)").bitcast(I32)

        def merge(c, copy):
            words = z_pairs[:].rearrange("p u n e -> p u (n e)").bitcast(U32)
            first = (c - 1) * CHUNK
            copy(
                z[c][:].bitcast(U32).rearrange("p (a i u) -> p a u i", i=RUN, u=PACK // PAIR),
                words[:, :, first : first + CHUNK].rearrange("p u (a i) -> p a u i", i=RUN),
            )

        def quantize_z(c):
            cols = slice(c * CHUNK, (c + 1) * CHUNK)
            nc.vector.quantize_mx(out=z_codes[:, cols].bitcast(FP8X4), scales=z_scale[:, cols], in_=z[c][:])

        def second_layer_pair(c, u, copy):
            second_layer(c, slice(PAIR * u, PAIR * (u + 1)), copy)

        def second_layer(c, groups, copy):
            cols = slice(c * CHUNK, (c + 1) * CHUNK)
            y_bank = psum.tile([P, groups.stop - groups.start, CHUNK], F32, name="bank", bufs=BANKS)
            for e, t in enumerate(range(groups.start, groups.stop)):
                nc.tensor.matmul_mx(
                    out=y_bank[:, e, :],
                    lhsT=w2_codes[:, 2 * t * P : 2 * (t + 1) * P].bitcast(FP4X4),
                    lhsT_scale=w2_scale[:, t * P : (t + 1) * P],
                    rhs=z_codes[:, cols].bitcast(FP8X4),
                    rhs_scale=z_scale[:, cols],
                    start=True,
                    stop=True,
                )
            copy(y[c][:, groups, :], y_bank[:])

        def regroup(c, copy):
            copy(
                y_grouped[c][:].rearrange("p (a i) t -> p a t i", i=RUN), y[c].rearrange("p t (a i) -> p a t i", i=RUN)
            )

        def quantize_y(c):
            cols = slice(c * CHUNK, (c + 1) * CHUNK)
            nc.vector.quantize_mx(
                out=y_codes[:, cols].bitcast(FP8X4),
                scales=y_scale[:, cols],
                in_=y_grouped[c][:].rearrange("p n t -> p (n t)"),
            )

        def store_y(c):
            nc.sync.dma_start(out_rows[:, :, c * CHUNK : (c + 1) * CHUNK], y[c])

        on_scalar, on_vector = nc.scalar.copy, nc.vector.tensor_copy

        centre(PACK - 1, slice(1, 2))
        centre(PACK - 1, slice(0, 1))
        merge(1, on_vector)
        quantize_z(0)
        centre(PACK - 1, slice(3, 4))
        for t in range(PAIR, PACK):
            centre_on_scalar(t, slice(2, 3))
        merge(2, on_scalar)
        for groups in (slice(0, 1), slice(1, 2), slice(2, 4)):
            second_layer(0, groups, on_scalar)
            nc.sync.dma_start(out_rows[:, groups, :CHUNK], y[0][:, groups, :])
        quantize_z(1)
        merge(3, on_vector)
        for c in (2, 3):
            quantize_z(c)
        second_layer_pair(1, 0, on_scalar)
        second_layer_pair(1, 1, on_vector)
        store_y(1)
        regroup(0, on_vector)
        for u, copies in enumerate(((on_scalar, on_vector), (on_scalar, on_scalar))):
            for c, copy in zip((2, 3), copies):
                second_layer_pair(c, u, copy)
            groups = slice(PAIR * u, PAIR * (u + 1))
            nc.sync.dma_start(out_rows[:, groups, 2 * CHUNK :], y_last[:, groups, :])
        quantize_y(0)
        regroup(1, on_vector)
        regroup(2, on_scalar)
        regroup(3, on_vector)
        for c in (1, 3, 2):
            quantize_y(c)
        nc.sync.dma_start(out_words, y_codes[:].bitcast(I32))
        for q in range(QUADRANTS):
            live = y_scale[QUADRANT * q : QUADRANT * q + ROWS, :]
            nc.scalar.dma_start(out_2[0, ROWS * q : ROWS * (q + 1), :].bitcast(I32), live.bitcast(I32))
